import numpy as np
import ml_dtypes


def mxq(x, axis, fmt="e4m3"):
    dtype, down = {"e4m3": (ml_dtypes.float8_e4m3fn, 7), "e5m2": (ml_dtypes.float8_e5m2, 14)}[fmt]
    v = np.moveaxis(np.asarray(x, np.float32).astype(ml_dtypes.bfloat16).astype(np.float64), axis, -1)
    blocks = v.reshape(v.shape[:-1] + (-1, 32))
    amax = np.abs(blocks).max(-1, keepdims=True)
    byte = np.maximum(np.where(amax > 0, np.frexp(amax)[1] - 1 + 127, 0) - down, 1)
    scale = np.exp2(byte - 127.0)
    codes = (blocks / scale).astype(np.float32).astype(dtype).astype(np.float64)
    return np.moveaxis((codes * scale).reshape(v.shape), -1, axis)


WIDE = False


def mx_kscale(k):
    if not WIDE:
        return np.ones(k)
    levels = np.array([24, -24, 12, -12, 0])
    if k % 512:
        return np.exp2(np.random.permutation(np.resize(levels, k // 32))).repeat(32)
    a = np.empty((k // 512, 16))
    for p in range(k // 512):
        a[p, :8] = np.random.permutation(np.resize(levels, 8))
        for g in range(8):
            far = levels[np.abs(levels - a[p, g]) >= 10]
            a[p, g + 8] = far[np.random.randint(len(far))]
    return np.exp2(a.ravel()).repeat(32)


def f64(x):
    return np.asarray(x).astype(np.float64)


def striped8(idx):
    return np.concatenate([v.reshape(-1, 16).T for v in idx]).astype(np.uint16)


def unstriped8(offs):
    return np.stack([offs[16 * g:16 * g + 16].T.reshape(-1) for g in range(8)]).astype(np.int64)


E2M1 = np.array([0.0, 0.5, 1.0, 1.5, 2.0, 3.0, 4.0, 6.0, -0.0, -0.5, -1.0, -1.5, -2.0, -3.0, -4.0, -6.0])


def pack_weight(w, fmt):
    k, n = w.shape
    w = f64(np.asarray(w, np.float32).astype(ml_dtypes.bfloat16)).reshape(k // 32, 32, n)
    amax = np.abs(w).max(1)
    if fmt == "e4m3":
        byte = np.frexp(amax)[1] - 1 + 127 - 7
    else:
        mant, ex = np.frexp(amax / 6.0)
        byte = np.where(mant > 0.5, ex, ex - 1) + 127
    byte = np.clip(np.where(amax > 0, byte, 1), 1, 254)
    scaled = (w * np.exp2(127.0 - byte)[:, None, :]).reshape(k, n).astype(np.float32)
    by_word = np.ascontiguousarray(scaled.reshape(k // 512, 128, 4, n).transpose(0, 1, 3, 2))
    if fmt == "e4m3":
        words = by_word.astype(ml_dtypes.float8_e4m3fn).view(np.uint8)
    else:
        c = by_word.astype(ml_dtypes.float4_e2m1fn).view(np.uint8) & 0xF
        words = (c[..., 0::2] | (c[..., 1::2] << 4)).reshape(k // 512, 128, 2 * n)
    return np.ascontiguousarray(words), np.ascontiguousarray(byte.astype(np.uint8).reshape(k // 512, 16, n))


def unpack_weight(words, scales, fmt):
    g, _, n = scales.shape
    words = np.ascontiguousarray(words).reshape(g, 128, n, -1)
    if fmt == "e4m3":
        vals = words.view(ml_dtypes.float8_e4m3fn).astype(np.float64)
    else:
        nib = np.empty((g, 128, n, 4), np.uint8)
        nib[..., 0::2] = words & 0xF
        nib[..., 1::2] = words >> 4
        vals = E2M1[nib]
    vals = vals * np.repeat(np.exp2(scales.astype(np.float64) - 127.0), 8, axis=1)[..., None]
    return vals.transpose(0, 1, 3, 2).reshape(g * 512, n)


def planes(y):
    n, m = y.shape
    v = y.astype(np.float32).astype(ml_dtypes.bfloat16).astype(np.float64).reshape(n // 32, 32, m)
    top = np.abs(v).max(1)
    byte = np.clip(np.where(top > 0, np.frexp(top)[1] - 1 + 127 - 7, 1), 1, 254)
    codes = (v * np.exp2(127.0 - byte)[:, None, :]).reshape(n, m).astype(np.float32).astype(ml_dtypes.float8_e4m3fn).view(np.uint8)
    words = codes.reshape(n // 512, 128, 4, m).transpose(0, 1, 3, 2)
    return np.ascontiguousarray(words), np.ascontiguousarray(byte.astype(np.uint8).reshape(n // 512, 16, m))


def sigm(f):
    return 1.0 / (1.0 + np.exp(-np.maximum(f, -700.0)))


K, N, T, J = 512, 512, 2048, 1024


def setup_inputs():
    n = np.random.standard_normal
    s = mx_kscale(K)[:, None]
    p_wk = pack_weight(n((K, N)) / np.sqrt(K) / s, "e2m1")
    p_wv4 = pack_weight(n((K, N)) / np.sqrt(K) / s, "e2m1")
    return {
        "xT": (n((K, T)) * s).astype(np.float32),
        "wgt": np.repeat(np.random.uniform(0.5, 2.0, (8, J)), 16, axis=0).astype(np.float32),
        "wk_words": p_wk[0],
        "wk_scales": p_wk[1],
        "wv4_words": p_wv4[0],
        "wv4_scales": p_wv4[1],
        "wvd": (0.4 * (n((K, N)) / np.sqrt(K) / s)).astype(np.float32),
        "st": (n((N, J))).astype(np.float32),
        "offs": striped8(np.stack([np.random.permutation(T)[:J] for _ in range(8)])),
    }


def reference(xT, wgt, wk_words, wk_scales, wv4_words, wv4_scales, wvd, st, offs):
    idx = unstriped8(offs)
    rows = np.arange(K)
    xg = f64(wgt)[rows // 4 % 128] * f64(xT)[rows[:, None], idx[rows % 512 // 64]]
    xT_ = mxq(xg, 0, "e4m3")
    wk_ = unpack_weight(wk_words, wk_scales, "e2m1")
    wv4_ = unpack_weight(wv4_words, wv4_scales, "e2m1")
    wvd_ = mxq(f64(wvd), 0, "e4m3")
    ke = wk_.T @ xT_
    ve = wv4_.T @ xT_ + wvd_.T @ xT_
    gate = sigm(ke * f64(st))
    out_0 = gate * ve
    return (out_0,) + planes(out_0)

@@ -1,0 +1,234 @@
+from contextlib import ExitStack
+
+import concourse.mybir as mybir
+
+K, N, T, J = 512, 512, 2048, 1024
+FLOPS = 3 * 2 * K * N * J
+
+F32 = mybir.dt.float32
+BF16 = mybir.dt.bfloat16
+I32 = mybir.dt.int32
+U32 = mybir.dt.uint32
+U16 = mybir.dt.uint16
+U8 = mybir.dt.uint8
+FP8X4 = mybir.dt.float8_e4m3fn_x4
+FP4X4 = mybir.dt.float4_e2m1fn_x4
+MULT = mybir.AluOpType.mult
+ADD = mybir.AluOpType.add
+SIGMOID = mybir.ActivationFunctionType.Sigmoid
+
+P = 128
+PACK = 4
+CHUNK = 256
+STEP = 128
+LIST_ROWS = 16
+
+
+def weave(t4):
+    return t4.rearrange("p t (c i) -> p c t i", i=4)
+
+
+def woven(bf):
+    return bf.rearrange("p (c i t) -> p c t i", i=4, t=PACK)
+
+
+def tile_list_dl_sigP_kernel(
+    tc, xT, wgt, wk_words, wk_scales, wv4_words, wv4_scales, wvd, st, offs, out_0, out_1, out_2
+):
+    nc = tc.nc
+    chunks = J // CHUNK
+    steps = J // STEP
+    x_rows = xT.rearrange("(p i) t -> p i t", i=PACK)
+    st_rows = st.rearrange("(p t) j -> p t j", t=PACK)
+    out_rows = out_0.rearrange("(p t) j -> p t j", t=PACK)
+    out_words = out_1[0].rearrange("p j i -> p (j i)").bitcast(I32)
+    out_scales = out_2[0].bitcast(I32)
+
+    with ExitStack() as ctx:
+        keep = ctx.enter_context(tc.tile_pool(name="keep", bufs=1))
+        ring = ctx.enter_context(tc.tile_pool(name="ring", bufs=4))
+        psum = ctx.enter_context(tc.psum_pool(name="psum", bufs=4))
+
+        warm = keep.tile([P, 1], F32, name="warm")
+        nc.vector.memset(warm[:], 0.0)
+        warm_out = keep.tile([P, 1], F32, name="warm_out")
+        nc.scalar.activation(out=warm_out[:], in_=warm[:], func=SIGMOID)
+
+        offsets = keep.tile([P, J // LIST_ROWS], U16, name="offsets")
+        raw_words = keep.tile([P, 2, 2 * N], U8, name="raw_words")
+        raw_scales = keep.tile([P, 2, N], U8, name="raw_scales")
+        planes = [keep.tile([P, T], F32, name="plane%d" % i) for i in range(PACK)]
+        weight = [keep.tile([P, J // 2], F32, name="weight%d" % h) for h in range(2)]
+        wvd_raw = keep.tile([P, PACK, N], F32, name="wvd_raw")
+        state = [keep.tile([P, PACK, CHUNK], F32, name="state%d" % c) for c in range(chunks)]
+
+        nc.gpsimd.memset(raw_scales[:].rearrange("p w n -> p (w n)").bitcast(I32), 0)
+
+        def load_scales(w, scales):
+            for q in range(4):
+                nc.sync.dma_start(
+                    out=raw_scales[32 * q : 32 * q + 4, w, :].bitcast(I32),
+                    in_=scales[0, 4 * q : 4 * q + 4, :].bitcast(I32),
+                )
+
+        def load_state(c):
+            nc.sync.dma_start(out=state[c][:], in_=st_rows[:, :, c * CHUNK : (c + 1) * CHUNK])
+
+        def load_wvd():
+            nc.sync.dma_start(out=wvd_raw[:], in_=wvd.rearrange("(p i) n -> p i n", i=PACK))
+
+        def load_plane(i):
+            nc.sync.dma_start(out=planes[i][:], in_=x_rows[:, i, :])
+
+        def load_weight(h):
+            nc.sync.dma_start(out=weight[h][:], in_=wgt[:, h * (J // 2) : (h + 1) * (J // 2)])
+
+        for w, words in enumerate((wk_words, wv4_words)):
+            nc.sync.dma_start(out=raw_words[:, w, :].bitcast(I32), in_=words[0].bitcast(I32))
+        nc.sync.dma_start(offsets[:], offs)
+        load_weight(0)
+        load_plane(0)
+        load_scales(0, wk_scales)
+        load_weight(1)
+        load_plane(1)
+        load_plane(2)
+        load_scales(1, wv4_scales)
+        load_plane(3)
+        load_wvd()
+        for c in range(chunks):
+            load_state(c)
+
+        w4_words = keep.tile([P, 2, 2 * N], U8, name="w4_words", align_bytes=64)
+        w4_scales = [keep.tile([P, N], U8, name="w4_scales%d" % w, align_bytes=64) for w in range(2)]
+        nc.vector.tensor_copy(
+            out=w4_words[:].rearrange("p w (t m b) -> p w t m b", t=PACK, b=2),
+            in_=raw_words[:].rearrange("p w (m t b) -> p w t m b", t=PACK, b=2),
+        )
+        for w in range(2):
+            nc.vector.tensor_copy(
+                out=w4_scales[w][:].rearrange("p (t m) -> p t m", t=PACK),
+                in_=raw_scales[:, w, :].rearrange("p (m t) -> p t m", t=PACK),
+            )
+
+        picked = [keep.tile([P, PACK, CHUNK], F32, name="picked%d" % c) for c in range(chunks)]
+        cols = CHUNK // LIST_ROWS
+        for i in range(PACK):
+            for c in range(chunks):
+                nc.vector.tensor_tensor(
+                    picked[c][:, i, :],
+                    planes[i][:].indirect(offsets[:, c * cols : (c + 1) * cols]),
+                    weight[c // 2][:, (c % 2) * CHUNK : (c % 2 + 1) * CHUNK],
+                    MULT,
+                )
+
+        xg_codes = [keep.tile([P, CHUNK], U32, name="xg_codes%d" % c, align_bytes=64) for c in range(chunks)]
+        xg_scales = [keep.tile([P, CHUNK], U8, name="xg_scales%d" % c, align_bytes=64) for c in range(chunks)]
+
+        def quantize_picks(c):
+            xg_bf = ring.tile([P, PACK * CHUNK], BF16, name="xg_bf", align_bytes=64)
+            nc.scalar.copy(out=woven(xg_bf[:]), in_=weave(picked[c][:]))
+            nc.vector.quantize_mx(out=xg_codes[c][:].bitcast(FP8X4), scales=xg_scales[c][:], in_=xg_bf[:])
+
+        wvd_bf = keep.tile([P, PACK * N], BF16, name="wvd_bf", align_bytes=64)
+        wvd_codes = keep.tile([P, N], U32, name="wvd_codes", align_bytes=64)
+        wvd_scales = keep.tile([P, N], U8, name="wvd_scales", align_bytes=64)
+
+        def quantize_wvd():
+            dst = wvd_bf[:].rearrange("p (t m i) -> p m t i", t=PACK, i=PACK)
+            src = wvd_raw[:].rearrange("p i (m t) -> p m t i", t=PACK)
+            nc.vector.tensor_copy(out=dst, in_=src)
+            nc.vector.quantize_mx(out=wvd_codes[:].bitcast(FP8X4), scales=wvd_scales[:], in_=wvd_bf[:])
+
+        y_codes = keep.tile([P, J], U32, name="y_codes", align_bytes=64)
+        y_scales = keep.tile([P, J], U8, name="y_scales", align_bytes=64)
+        y = [keep.tile([P, PACK, CHUNK], F32, name="y%d" % c) for c in range(chunks)]
+        gates = {}
+
+        def operand(s):
+            c, h = divmod(s, CHUNK // STEP)
+            cs = slice(h * STEP, (h + 1) * STEP)
+            return c, cs, xg_codes[c][:, cs].bitcast(FP8X4), xg_scales[c][:, cs]
+
+        def gate_step(s):
+            c, cs, rhs, rhs_scale = operand(s)
+            ke = psum.tile([P, PACK, STEP], F32, name="ke")
+            for t in range(PACK):
+                nc.tensor.matmul_mx(
+                    out=ke[:, t, :],
+                    lhsT=w4_words[:, 0, 2 * P * t : 2 * P * (t + 1)].bitcast(FP4X4),
+                    lhsT_scale=w4_scales[0][:, P * t : P * (t + 1)],
+                    rhs=rhs, rhs_scale=rhs_scale, start=True, stop=True,
+                )
+            z = ring.tile([P, PACK, STEP], F32, name="z")
+            nc.vector.tensor_tensor(z[:], ke[:], state[c][:, :, cs], MULT)
+            gate = ring.tile([P, PACK, STEP], F32, name="gate")
+            nc.scalar.activation(out=gate[:], in_=z[:], func=SIGMOID)
+            gates[s] = gate
+
+        def value_step(s):
+            c, cs, rhs, rhs_scale = operand(s)
+            ve = psum.tile([P, PACK, STEP], F32, name="ve")
+            for t in range(PACK):
+                nc.tensor.matmul_mx(
+                    out=ve[:, t, :],
+                    lhsT=w4_words[:, 1, 2 * P * t : 2 * P * (t + 1)].bitcast(FP4X4),
+                    lhsT_scale=w4_scales[1][:, P * t : P * (t + 1)],
+                    rhs=rhs, rhs_scale=rhs_scale, start=True, stop=False,
+                )
+                nc.tensor.matmul_mx(
+                    out=ve[:, t, :],
+                    lhsT=wvd_codes[:, P * t : P * (t + 1)].bitcast(FP8X4),
+                    lhsT_scale=wvd_scales[:, P * t : P * (t + 1)],
+                    rhs=rhs, rhs_scale=rhs_scale, start=False, stop=True,
+                )
+            nc.vector.tensor_tensor(y[c][:, :, cs], ve[:], gates[s][:], MULT)
+
+        y_bf = {}
+
+        def round_step(s):
+            c, cs = operand(s)[:2]
+            bf = ring.tile([P, PACK * STEP], BF16, name="y_bf", align_bytes=64)
+            dst = woven(bf[:])
+            src = weave(y[c][:, :, cs])
+            nc.scalar.copy(out=dst, in_=src)
+            y_bf[s] = bf
+
+        def plane_step(s):
+            js = slice(s * STEP, (s + 1) * STEP)
+            nc.vector.quantize_mx(out=y_codes[:, js].bitcast(FP8X4), scales=y_scales[:, js], in_=y_bf[s][:])
+
+        def store(c, lo, hi):
+            nc.sync.dma_start(out=out_rows[:, :, c * CHUNK + lo : c * CHUNK + hi], in_=y[c][:, :, lo:hi])
+
+        def store_words(j0, j1):
+            nc.sync.dma_start(out=out_words[:, j0:j1], in_=y_codes[:, j0:j1].bitcast(I32))
+
+        quantize_picks(0)
+        quantize_wvd()
+        quantize_picks(1)
+        for s in range(steps + 3):
+            if s < steps:
+                gate_step(s)
+            if s in (1, 3):
+                quantize_picks(2 + s // 2)
+            if 1 <= s < steps + 1:
+                value_step(s - 1)
+                if s - 1 >= steps - 2:
+                    store(chunks - 1, (s - 1) % 2 * STEP, ((s - 1) % 2 + 1) * STEP)
+                elif s % 2 == 0:
+                    store((s - 1) // 2, 0, CHUNK)
+            if 2 <= s < steps + 2:
+                round_step(s - 2)
+            if 3 <= s:
+                plane_step(s - 3)
+                if s - 3 == 3:
+                    store_words(0, 4 * STEP)
+                if s - 3 == 6:
+                    store_words(4 * STEP, 7 * STEP)
+                if s - 3 == 7:
+                    store_words(7 * STEP, 8 * STEP)
+        for q in range(4):
+            eng = nc.sync if q % 2 == 0 else nc.scalar
+            eng.dma_start(
+                out=out_scales[4 * q : 4 * q + 4, :], in_=y_scales[32 * q : 32 * q + 4, :].bitcast(I32)
+            )

@@ -25,11 +25,11 @@ LIST_ROWS = 16
 
 
 def weave(t4):
-    return t4.rearrange("p t (c i) -> p c t i", i=4)
+    return t4.rearrange("p t (c i) -> p c t i", i=2)
 
 
 def woven(bf):
-    return bf.rearrange("p (c i t) -> p c t i", i=4, t=PACK)
+    return bf.rearrange("p (c i t) -> p c t i", i=2, t=PACK)
 
 
 def tile_list_dl_sigP_kernel(
@@ -134,8 +134,8 @@ def tile_list_dl_sigP_kernel(
         wvd_scales = keep.tile([P, N], U8, name="wvd_scales", align_bytes=64)
 
         def quantize_wvd():
-            dst = wvd_bf[:].rearrange("p (t m i) -> p m t i", t=PACK, i=PACK)
-            src = wvd_raw[:].rearrange("p i (m t) -> p m t i", t=PACK)
+            dst = wvd_bf[:].rearrange("p (u e m i) -> p u m i e", u=2, e=2, i=PACK)
+            src = wvd_raw[:].rearrange("p i (m u e) -> p u m i e", u=2, e=2)
             nc.vector.tensor_copy(out=dst, in_=src)
             nc.vector.quantize_mx(out=wvd_codes[:].bitcast(FP8X4), scales=wvd_scales[:], in_=wvd_bf[:])
 

@@ -58,7 +58,7 @@ def tile_list_dl_sigP_kernel(
         raw_words = keep.tile([P, 2, 2 * N], U8, name="raw_words")
         raw_scales = keep.tile([P, 2, N], U8, name="raw_scales")
         planes = [keep.tile([P, T], F32, name="plane%d" % i) for i in range(PACK)]
-        weight = [keep.tile([P, J // 2], F32, name="weight%d" % h) for h in range(2)]
+        weight = keep.tile([P, J], F32, name="weight")
         wvd_raw = keep.tile([P, PACK, N], F32, name="wvd_raw")
         state = [keep.tile([P, PACK, CHUNK], F32, name="state%d" % c) for c in range(chunks)]
 
@@ -81,18 +81,18 @@ def tile_list_dl_sigP_kernel(
             nc.sync.dma_start(out=planes[i][:], in_=x_rows[:, i, :])
 
         def load_weight(h):
-            nc.sync.dma_start(out=weight[h][:], in_=wgt[:, h * (J // 2) : (h + 1) * (J // 2)])
+            nc.sync.dma_start(out=weight[:, h * (J // 2) : (h + 1) * (J // 2)], in_=wgt[:, h * (J // 2) : (h + 1) * (J // 2)])
 
-        for w, words in enumerate((wk_words, wv4_words)):
-            nc.sync.dma_start(out=raw_words[:, w, :].bitcast(I32), in_=words[0].bitcast(I32))
         nc.sync.dma_start(offsets[:], offs)
         load_weight(0)
         load_plane(0)
         load_scales(0, wk_scales)
         load_weight(1)
         load_plane(1)
-        load_plane(2)
+        for w, words in enumerate((wk_words, wv4_words)):
+            nc.sync.dma_start(out=raw_words[:, w, :].bitcast(I32), in_=words[0].bitcast(I32))
         load_scales(1, wv4_scales)
+        load_plane(2)
         load_plane(3)
         load_wvd()
         for c in range(chunks):
@@ -100,33 +100,46 @@ def tile_list_dl_sigP_kernel(
 
         w4_words = keep.tile([P, 2, 2 * N], U8, name="w4_words", align_bytes=64)
         w4_scales = [keep.tile([P, N], U8, name="w4_scales%d" % w, align_bytes=64) for w in range(2)]
-        nc.vector.tensor_copy(
-            out=w4_words[:].rearrange("p w (t m b) -> p w t m b", t=PACK, b=2),
-            in_=raw_words[:].rearrange("p w (m t b) -> p w t m b", t=PACK, b=2),
-        )
-        for w in range(2):
+
+        def deal_words():
+            nc.vector.tensor_copy(
+                out=w4_words[:].bitcast(U16).rearrange("p w (t m) -> p w t m", t=PACK),
+                in_=raw_words[:].bitcast(U16).rearrange("p w (m t) -> p w t m", t=PACK),
+            )
+
+        def deal_scales(w):
             nc.vector.tensor_copy(
                 out=w4_scales[w][:].rearrange("p (t m) -> p t m", t=PACK),
                 in_=raw_scales[:, w, :].rearrange("p (m t) -> p t m", t=PACK),
             )
 
-        picked = [keep.tile([P, PACK, CHUNK], F32, name="picked%d" % c) for c in range(chunks)]
+        picked = keep.tile([P, PACK, J], F32, name="picked")
         cols = CHUNK // LIST_ROWS
-        for i in range(PACK):
-            for c in range(chunks):
-                nc.vector.tensor_tensor(
-                    picked[c][:, i, :],
-                    planes[i][:].indirect(offsets[:, c * cols : (c + 1) * cols]),
-                    weight[c // 2][:, (c % 2) * CHUNK : (c % 2 + 1) * CHUNK],
-                    MULT,
-                )
+
+        def gather(i, c0, c1):
+            nc.vector.tensor_tensor(
+                picked[:, i, c0 * CHUNK : c1 * CHUNK],
+                planes[i][:].indirect(offsets[:, c0 * cols : c1 * cols]),
+                weight[:, c0 * CHUNK : c1 * CHUNK],
+                MULT,
+            )
+
+        gather(0, 0, 2)
+        deal_scales(0)
+        gather(0, 2, chunks)
+        gather(1, 0, chunks)
+        deal_words()
+        deal_scales(1)
+        gather(2, 0, chunks)
+        for c in range(chunks):
+            gather(3, c, c + 1)
 
         xg_codes = [keep.tile([P, CHUNK], U32, name="xg_codes%d" % c, align_bytes=64) for c in range(chunks)]
         xg_scales = [keep.tile([P, CHUNK], U8, name="xg_scales%d" % c, align_bytes=64) for c in range(chunks)]
 
         def quantize_picks(c):
             xg_bf = ring.tile([P, PACK * CHUNK], BF16, name="xg_bf", align_bytes=64)
-            nc.scalar.copy(out=woven(xg_bf[:]), in_=weave(picked[c][:]))
+            nc.scalar.copy(out=woven(xg_bf[:]), in_=weave(picked[:, :, c * CHUNK : (c + 1) * CHUNK]))
             nc.vector.quantize_mx(out=xg_codes[c][:].bitcast(FP8X4), scales=xg_scales[c][:], in_=xg_bf[:])
 
         wvd_bf = keep.tile([P, PACK * N], BF16, name="wvd_bf", align_bytes=64)
@@ -143,6 +156,7 @@ def tile_list_dl_sigP_kernel(
         y_scales = keep.tile([P, J], U8, name="y_scales", align_bytes=64)
         y = [keep.tile([P, PACK, CHUNK], F32, name="y%d" % c) for c in range(chunks)]
         gates = {}
+        y_bf = [keep.tile([P, PACK * CHUNK], BF16, name="y_bf%d" % c, align_bytes=64) for c in range(chunks)]
 
         def operand(s):
             c, h = divmod(s, CHUNK // STEP)
@@ -182,51 +196,48 @@ def tile_list_dl_sigP_kernel(
                     rhs=rhs, rhs_scale=rhs_scale, start=False, stop=True,
                 )
             nc.vector.tensor_tensor(y[c][:, :, cs], ve[:], gates[s][:], MULT)
+            if s == steps - 1:
+                nc.vector.tensor_tensor(woven(y_bf[c][:, PACK * STEP :]), weave(ve[:]), weave(gates[s][:]), MULT)
 
-        y_bf = {}
+        def round_cols(c, lo, hi):
+            nc.scalar.copy(out=woven(y_bf[c][:, PACK * lo : PACK * hi]), in_=weave(y[c][:, :, lo:hi]))
 
-        def round_step(s):
-            c, cs = operand(s)[:2]
-            bf = ring.tile([P, PACK * STEP], BF16, name="y_bf", align_bytes=64)
-            dst = woven(bf[:])
-            src = weave(y[c][:, :, cs])
-            nc.scalar.copy(out=dst, in_=src)
-            y_bf[s] = bf
-
-        def plane_step(s):
-            js = slice(s * STEP, (s + 1) * STEP)
-            nc.vector.quantize_mx(out=y_codes[:, js].bitcast(FP8X4), scales=y_scales[:, js], in_=y_bf[s][:])
+        def plane_cols(c, lo, hi):
+            js = slice(c * CHUNK + lo, c * CHUNK + hi)
+            nc.vector.quantize_mx(
+                out=y_codes[:, js].bitcast(FP8X4), scales=y_scales[:, js], in_=y_bf[c][:, PACK * lo : PACK * hi]
+            )
 
         def store(c, lo, hi):
             nc.sync.dma_start(out=out_rows[:, :, c * CHUNK + lo : c * CHUNK + hi], in_=y[c][:, :, lo:hi])
 
-        def store_words(j0, j1):
-            nc.sync.dma_start(out=out_words[:, j0:j1], in_=y_codes[:, j0:j1].bitcast(I32))
+        def store_words(j0, j1, eng=nc.sync):
+            eng.dma_start(out=out_words[:, j0:j1], in_=y_codes[:, j0:j1].bitcast(I32))
 
         quantize_picks(0)
         quantize_wvd()
         quantize_picks(1)
-        for s in range(steps + 3):
+        last = chunks - 1
+        for s in range(steps + 1):
             if s < steps:
                 gate_step(s)
             if s in (1, 3):
                 quantize_picks(2 + s // 2)
-            if 1 <= s < steps + 1:
+            if 1 <= s:
+                c, h = divmod(s - 1, 2)
                 value_step(s - 1)
-                if s - 1 >= steps - 2:
-                    store(chunks - 1, (s - 1) % 2 * STEP, ((s - 1) % 2 + 1) * STEP)
-                elif s % 2 == 0:
-                    store((s - 1) // 2, 0, CHUNK)
-            if 2 <= s < steps + 2:
-                round_step(s - 2)
-            if 3 <= s:
-                plane_step(s - 3)
-                if s - 3 == 3:
-                    store_words(0, 4 * STEP)
-                if s - 3 == 6:
-                    store_words(4 * STEP, 7 * STEP)
-                if s - 3 == 7:
-                    store_words(7 * STEP, 8 * STEP)
+                if c == last:
+                    store(c, h * STEP, (h + 1) * STEP)
+                    if h == 0:
+                        round_cols(c, 0, STEP)
+                elif h == 1:
+                    store(c, 0, CHUNK)
+                    round_cols(c, 0, CHUNK)
+                if h == 0 and c > 0:
+                    plane_cols(c - 1, 0, CHUNK)
+                    store_words((c - 1) * CHUNK, c * CHUNK)
+        plane_cols(last, 0, CHUNK)
+        store_words(last * CHUNK, J, nc.scalar)
         for q in range(4):
             eng = nc.sync if q % 2 == 0 else nc.scalar
             eng.dma_start(

@@ -197,7 +197,14 @@ def tile_list_dl_sigP_kernel(
                 )
             nc.vector.tensor_tensor(y[c][:, :, cs], ve[:], gates[s][:], MULT)
             if s == steps - 1:
-                nc.vector.tensor_tensor(woven(y_bf[c][:, PACK * STEP :]), weave(ve[:]), weave(gates[s][:]), MULT)
+                half = STEP // 2
+                round_cols(c, STEP, STEP + half)
+                nc.vector.tensor_tensor(
+                    woven(y_bf[c][:, PACK * (STEP + half) :]),
+                    weave(ve[:, :, half:]),
+                    weave(gates[s][:, :, half:]),
+                    MULT,
+                )
 
         def round_cols(c, lo, hi):
             nc.scalar.copy(out=woven(y_bf[c][:, PACK * lo : PACK * hi]), in_=weave(y[c][:, :, lo:hi]))
@@ -218,25 +225,26 @@ def tile_list_dl_sigP_kernel(
         quantize_wvd()
         quantize_picks(1)
         last = chunks - 1
-        for s in range(steps + 1):
-            if s < steps:
-                gate_step(s)
-            if s in (1, 3):
-                quantize_picks(2 + s // 2)
-            if 1 <= s:
-                c, h = divmod(s - 1, 2)
-                value_step(s - 1)
-                if c == last:
-                    store(c, h * STEP, (h + 1) * STEP)
-                    if h == 0:
-                        round_cols(c, 0, STEP)
-                elif h == 1:
-                    store(c, 0, CHUNK)
-                    round_cols(c, 0, CHUNK)
-                if h == 0 and c > 0:
-                    plane_cols(c - 1, 0, CHUNK)
-                    store_words((c - 1) * CHUNK, c * CHUNK)
-        plane_cols(last, 0, CHUNK)
+        gate_step(0)
+        gate_step(1)
+        for s in range(steps):
+            c, h = divmod(s, 2)
+            if s + 2 < steps:
+                if h == 0 and c + 2 < chunks:
+                    quantize_picks(c + 2)
+                gate_step(s + 2)
+            value_step(s)
+            if c >= last - 1:
+                store(c, h * STEP, (h + 1) * STEP)
+            elif h == 1:
+                store(c, 0, CHUNK)
+            if s < steps - 1:
+                round_cols(c, h * STEP, (h + 1) * STEP)
+            if h == 0 and c > 0:
+                plane_cols(c - 1, 0, CHUNK)
+                store_words((c - 1) * CHUNK, c * CHUNK)
+        plane_cols(last, 0, STEP)
+        plane_cols(last, STEP, CHUNK)
         store_words(last * CHUNK, J, nc.scalar)
         for q in range(4):
             eng = nc.sync if q % 2 == 0 else nc.scalar

@@ -14,22 +14,25 @@ U8 = mybir.dt.uint8
 FP8X4 = mybir.dt.float8_e4m3fn_x4
 FP4X4 = mybir.dt.float4_e2m1fn_x4
 MULT = mybir.AluOpType.mult
-ADD = mybir.AluOpType.add
 SIGMOID = mybir.ActivationFunctionType.Sigmoid
 
 P = 128
 PACK = 4
-CHUNK = 256
-STEP = 128
+QUADRANTS = 4
 LIST_ROWS = 16
+BANK = 512
+CHUNK = 256
+NARROW = 128
+DEPTH = 4
+LEAD = 2
 
 
-def weave(t4):
-    return t4.rearrange("p t (c i) -> p c t i", i=2)
+def weave(rows):
+    return rows.rearrange("p t (c e) -> p c t e", e=2)
 
 
-def woven(bf):
-    return bf.rearrange("p (c i t) -> p c t i", i=2, t=PACK)
+def woven(packed):
+    return packed.rearrange("p (c e t) -> p c t e", e=2, t=PACK)
 
 
 def tile_list_dl_sigP_kernel(
@@ -37,7 +40,8 @@ def tile_list_dl_sigP_kernel(
 ):
     nc = tc.nc
     chunks = J // CHUNK
-    steps = J // STEP
+    steps = 2 * chunks
+    last = chunks - 1
     x_rows = xT.rearrange("(p i) t -> p i t", i=PACK)
     st_rows = st.rearrange("(p t) j -> p t j", t=PACK)
     out_rows = out_0.rearrange("(p t) j -> p t j", t=PACK)
@@ -46,8 +50,8 @@ def tile_list_dl_sigP_kernel(
 
     with ExitStack() as ctx:
         keep = ctx.enter_context(tc.tile_pool(name="keep", bufs=1))
-        ring = ctx.enter_context(tc.tile_pool(name="ring", bufs=4))
-        psum = ctx.enter_context(tc.psum_pool(name="psum", bufs=4))
+        ring = ctx.enter_context(tc.tile_pool(name="ring", bufs=DEPTH))
+        psum = ctx.enter_context(tc.psum_pool(name="psum", bufs=DEPTH))
 
         warm = keep.tile([P, 1], F32, name="warm")
         nc.vector.memset(warm[:], 0.0)
@@ -65,38 +69,32 @@ def tile_list_dl_sigP_kernel(
         nc.gpsimd.memset(raw_scales[:].rearrange("p w n -> p (w n)").bitcast(I32), 0)
 
         def load_scales(w, scales):
-            for q in range(4):
+            for q in range(QUADRANTS):
                 nc.sync.dma_start(
                     out=raw_scales[32 * q : 32 * q + 4, w, :].bitcast(I32),
                     in_=scales[0, 4 * q : 4 * q + 4, :].bitcast(I32),
                 )
 
-        def load_state(c):
-            nc.sync.dma_start(out=state[c][:], in_=st_rows[:, :, c * CHUNK : (c + 1) * CHUNK])
-
-        def load_wvd():
-            nc.sync.dma_start(out=wvd_raw[:], in_=wvd.rearrange("(p i) n -> p i n", i=PACK))
-
         def load_plane(i):
             nc.sync.dma_start(out=planes[i][:], in_=x_rows[:, i, :])
 
-        def load_weight(h):
-            nc.sync.dma_start(out=weight[:, h * (J // 2) : (h + 1) * (J // 2)], in_=wgt[:, h * (J // 2) : (h + 1) * (J // 2)])
+        def load_weight(j0, j1):
+            nc.sync.dma_start(out=weight[:, j0:j1], in_=wgt[:, j0:j1])
 
         nc.sync.dma_start(offsets[:], offs)
-        load_weight(0)
+        load_weight(0, J // 2)
         load_plane(0)
         load_scales(0, wk_scales)
-        load_weight(1)
+        load_weight(J // 2, J)
         load_plane(1)
         for w, words in enumerate((wk_words, wv4_words)):
             nc.sync.dma_start(out=raw_words[:, w, :].bitcast(I32), in_=words[0].bitcast(I32))
         load_scales(1, wv4_scales)
         load_plane(2)
         load_plane(3)
-        load_wvd()
+        nc.sync.dma_start(out=wvd_raw[:], in_=wvd.rearrange("(p i) n -> p i n", i=PACK))
         for c in range(chunks):
-            load_state(c)
+            nc.sync.dma_start(out=state[c][:], in_=st_rows[:, :, c * CHUNK : (c + 1) * CHUNK])
 
         w4_words = keep.tile([P, 2, 2 * N], U8, name="w4_words", align_bytes=64)
         w4_scales = [keep.tile([P, N], U8, name="w4_scales%d" % w, align_bytes=64) for w in range(2)]
@@ -114,25 +112,24 @@ def tile_list_dl_sigP_kernel(
             )
 
         picked = keep.tile([P, PACK, J], F32, name="picked")
-        cols = CHUNK // LIST_ROWS
 
-        def gather(i, c0, c1):
+        def gather(i, j0, j1):
             nc.vector.tensor_tensor(
-                picked[:, i, c0 * CHUNK : c1 * CHUNK],
-                planes[i][:].indirect(offsets[:, c0 * cols : c1 * cols]),
-                weight[:, c0 * CHUNK : c1 * CHUNK],
+                picked[:, i, j0:j1],
+                planes[i][:].indirect(offsets[:, j0 // LIST_ROWS : j1 // LIST_ROWS]),
+                weight[:, j0:j1],
                 MULT,
             )
 
-        gather(0, 0, 2)
+        gather(0, 0, J // 2)
         deal_scales(0)
-        gather(0, 2, chunks)
-        gather(1, 0, chunks)
+        gather(0, J // 2, J)
+        gather(1, 0, J)
         deal_words()
         deal_scales(1)
-        gather(2, 0, chunks)
+        gather(2, 0, J)
         for c in range(chunks):
-            gather(3, c, c + 1)
+            gather(3, c * CHUNK, (c + 1) * CHUNK)
 
         xg_codes = [keep.tile([P, CHUNK], U32, name="xg_codes%d" % c, align_bytes=64) for c in range(chunks)]
         xg_scales = [keep.tile([P, CHUNK], U8, name="xg_scales%d" % c, align_bytes=64) for c in range(chunks)]
@@ -147,107 +144,116 @@ def tile_list_dl_sigP_kernel(
         wvd_scales = keep.tile([P, N], U8, name="wvd_scales", align_bytes=64)
 
         def quantize_wvd():
-            dst = wvd_bf[:].rearrange("p (u e m i) -> p u m i e", u=2, e=2, i=PACK)
-            src = wvd_raw[:].rearrange("p i (m u e) -> p u m i e", u=2, e=2)
-            nc.vector.tensor_copy(out=dst, in_=src)
+            nc.vector.tensor_copy(
+                out=wvd_bf[:].rearrange("p (u e m i) -> p u m i e", u=2, e=2, i=PACK),
+                in_=wvd_raw[:].rearrange("p i (m u e) -> p u m i e", u=2, e=2),
+            )
             nc.vector.quantize_mx(out=wvd_codes[:].bitcast(FP8X4), scales=wvd_scales[:], in_=wvd_bf[:])
 
         y_codes = keep.tile([P, J], U32, name="y_codes", align_bytes=64)
         y_scales = keep.tile([P, J], U8, name="y_scales", align_bytes=64)
         y = [keep.tile([P, PACK, CHUNK], F32, name="y%d" % c) for c in range(chunks)]
-        gates = {}
         y_bf = [keep.tile([P, PACK * CHUNK], BF16, name="y_bf%d" % c, align_bytes=64) for c in range(chunks)]
+        gates = {}
 
-        def operand(s):
-            c, h = divmod(s, CHUNK // STEP)
-            cs = slice(h * STEP, (h + 1) * STEP)
-            return c, cs, xg_codes[c][:, cs].bitcast(FP8X4), xg_scales[c][:, cs]
+        def part(s):
+            c, h = divmod(s, 2)
+            if c == last:
+                return c, range(PACK), slice(h * NARROW, (h + 1) * NARROW)
+            return c, range(2 * h, 2 * h + 2), slice(0, CHUNK)
+
+        def by_slice(tile, ts):
+            return tile[:].rearrange("p (t j) -> p t j", t=len(ts))
 
         def gate_step(s):
-            c, cs, rhs, rhs_scale = operand(s)
-            ke = psum.tile([P, PACK, STEP], F32, name="ke")
-            for t in range(PACK):
+            c, ts, cs = part(s)
+            ke_bank = psum.tile([P, BANK], F32, name="ke")
+            ke = by_slice(ke_bank, ts)
+            for t in ts:
                 nc.tensor.matmul_mx(
-                    out=ke[:, t, :],
+                    out=ke[:, t - ts.start, :],
                     lhsT=w4_words[:, 0, 2 * P * t : 2 * P * (t + 1)].bitcast(FP4X4),
                     lhsT_scale=w4_scales[0][:, P * t : P * (t + 1)],
-                    rhs=rhs, rhs_scale=rhs_scale, start=True, stop=True,
+                    rhs=xg_codes[c][:, cs].bitcast(FP8X4),
+                    rhs_scale=xg_scales[c][:, cs],
+                    start=True,
+                    stop=True,
                 )
-            z = ring.tile([P, PACK, STEP], F32, name="z")
-            nc.vector.tensor_tensor(z[:], ke[:], state[c][:, :, cs], MULT)
-            gate = ring.tile([P, PACK, STEP], F32, name="gate")
+            z = ring.tile([P, BANK], F32, name="z")
+            nc.vector.tensor_tensor(by_slice(z, ts), ke, state[c][:, ts.start : ts.stop, cs], MULT)
+            gate = ring.tile([P, BANK], F32, name="gate")
             nc.scalar.activation(out=gate[:], in_=z[:], func=SIGMOID)
-            gates[s] = gate
+            gates[s] = by_slice(gate, ts)
 
         def value_step(s):
-            c, cs, rhs, rhs_scale = operand(s)
-            ve = psum.tile([P, PACK, STEP], F32, name="ve")
-            for t in range(PACK):
-                nc.tensor.matmul_mx(
-                    out=ve[:, t, :],
-                    lhsT=w4_words[:, 1, 2 * P * t : 2 * P * (t + 1)].bitcast(FP4X4),
-                    lhsT_scale=w4_scales[1][:, P * t : P * (t + 1)],
-                    rhs=rhs, rhs_scale=rhs_scale, start=True, stop=False,
-                )
-                nc.tensor.matmul_mx(
-                    out=ve[:, t, :],
-                    lhsT=wvd_codes[:, P * t : P * (t + 1)].bitcast(FP8X4),
-                    lhsT_scale=wvd_scales[:, P * t : P * (t + 1)],
-                    rhs=rhs, rhs_scale=rhs_scale, start=False, stop=True,
-                )
-            nc.vector.tensor_tensor(y[c][:, :, cs], ve[:], gates[s][:], MULT)
-            if s == steps - 1:
-                half = STEP // 2
-                round_cols(c, STEP, STEP + half)
-                nc.vector.tensor_tensor(
-                    woven(y_bf[c][:, PACK * (STEP + half) :]),
-                    weave(ve[:, :, half:]),
-                    weave(gates[s][:, :, half:]),
-                    MULT,
-                )
+            c, ts, cs = part(s)
+            ve_bank = psum.tile([P, BANK], F32, name="ve")
+            ve = by_slice(ve_bank, ts)
+            for t in ts:
+                for j0 in range(cs.start, cs.stop, NARROW):
+                    js = slice(j0, j0 + NARROW)
+                    acc = ve[:, t - ts.start, j0 - cs.start : j0 - cs.start + NARROW]
+                    rhs, rhs_scale = xg_codes[c][:, js].bitcast(FP8X4), xg_scales[c][:, js]
+                    nc.tensor.matmul_mx(
+                        out=acc,
+                        lhsT=w4_words[:, 1, 2 * P * t : 2 * P * (t + 1)].bitcast(FP4X4),
+                        lhsT_scale=w4_scales[1][:, P * t : P * (t + 1)],
+                        rhs=rhs,
+                        rhs_scale=rhs_scale,
+                        start=True,
+                        stop=False,
+                    )
+                    nc.tensor.matmul_mx(
+                        out=acc,
+                        lhsT=wvd_codes[:, P * t : P * (t + 1)].bitcast(FP8X4),
+                        lhsT_scale=wvd_scales[:, P * t : P * (t + 1)],
+                        rhs=rhs,
+                        rhs_scale=rhs_scale,
+                        start=False,
+                        stop=True,
+                    )
+            result = y[c][:, ts.start : ts.stop, cs]
+            nc.vector.tensor_tensor(result, ve, gates[s], MULT)
+            nc.sync.dma_start(
+                out=out_rows[:, ts.start : ts.stop, c * CHUNK + cs.start : c * CHUNK + cs.stop], in_=result
+            )
 
-        def round_cols(c, lo, hi):
-            nc.scalar.copy(out=woven(y_bf[c][:, PACK * lo : PACK * hi]), in_=weave(y[c][:, :, lo:hi]))
+        def round_result(c, lo, hi, copy):
+            copy(out=woven(y_bf[c][:, PACK * lo : PACK * hi]), in_=weave(y[c][:, :, lo:hi]))
 
-        def plane_cols(c, lo, hi):
+        def quantize_result(c, lo, hi):
             js = slice(c * CHUNK + lo, c * CHUNK + hi)
             nc.vector.quantize_mx(
                 out=y_codes[:, js].bitcast(FP8X4), scales=y_scales[:, js], in_=y_bf[c][:, PACK * lo : PACK * hi]
             )
 
-        def store(c, lo, hi):
-            nc.sync.dma_start(out=out_rows[:, :, c * CHUNK + lo : c * CHUNK + hi], in_=y[c][:, :, lo:hi])
-
-        def store_words(j0, j1, eng=nc.sync):
-            eng.dma_start(out=out_words[:, j0:j1], in_=y_codes[:, j0:j1].bitcast(I32))
+        def store_codes(c, queue):
+            js = slice(c * CHUNK, (c + 1) * CHUNK)
+            queue.dma_start(out=out_words[:, js], in_=y_codes[:, js].bitcast(I32))
 
         quantize_picks(0)
         quantize_wvd()
         quantize_picks(1)
-        last = chunks - 1
-        gate_step(0)
-        gate_step(1)
+        for s in range(LEAD):
+            gate_step(s)
         for s in range(steps):
             c, h = divmod(s, 2)
-            if s + 2 < steps:
+            if s + LEAD < steps:
                 if h == 0 and c + 2 < chunks:
                     quantize_picks(c + 2)
-                gate_step(s + 2)
+                gate_step(s + LEAD)
             value_step(s)
-            if c >= last - 1:
-                store(c, h * STEP, (h + 1) * STEP)
+            if c == last:
+                round_result(c, h * NARROW, (h + 1) * NARROW, nc.vector.tensor_copy if h == 1 else nc.scalar.copy)
             elif h == 1:
-                store(c, 0, CHUNK)
-            if s < steps - 1:
-                round_cols(c, h * STEP, (h + 1) * STEP)
+                round_result(c, 0, CHUNK, nc.scalar.copy)
             if h == 0 and c > 0:
-                plane_cols(c - 1, 0, CHUNK)
-                store_words((c - 1) * CHUNK, c * CHUNK)
-        plane_cols(last, 0, STEP)
-        plane_cols(last, STEP, CHUNK)
-        store_words(last * CHUNK, J, nc.scalar)
-        for q in range(4):
-            eng = nc.sync if q % 2 == 0 else nc.scalar
-            eng.dma_start(
-                out=out_scales[4 * q : 4 * q + 4, :], in_=y_scales[32 * q : 32 * q + 4, :].bitcast(I32)
-            )
+                quantize_result(c - 1, 0, CHUNK)
+                store_codes(c - 1, nc.sync)
+        quantize_result(last, 0, NARROW)
+        quantize_result(last, NARROW, CHUNK)
+
+        store_codes(last, nc.scalar)
+        for q in range(QUADRANTS):
+            queue = nc.sync if q % 2 == 0 else nc.scalar
+            queue.dma_start(out=out_scales[4 * q : 4 * q + 4, :], in_=y_scales[32 * q : 32 * q + 4, :].bitcast(I32))

@@ -1,6 +1,7 @@
 from contextlib import ExitStack
 
 import concourse.mybir as mybir
+from concourse.masks import make_identity
 
 K, N, T, J = 512, 512, 2048, 1024
 FLOPS = 3 * 2 * K * N * J
@@ -24,7 +25,7 @@ BANK = 512
 CHUNK = 256
 NARROW = 128
 DEPTH = 4
-LEAD = 2
+LEAD = 4
 
 
 def weave(rows):
@@ -53,24 +54,23 @@ def tile_list_dl_sigP_kernel(
         ring = ctx.enter_context(tc.tile_pool(name="ring", bufs=DEPTH))
         psum = ctx.enter_context(tc.psum_pool(name="psum", bufs=DEPTH))
 
-        warm = keep.tile([P, 1], F32, name="warm")
-        nc.vector.memset(warm[:], 0.0)
-        warm_out = keep.tile([P, 1], F32, name="warm_out")
-        nc.scalar.activation(out=warm_out[:], in_=warm[:], func=SIGMOID)
-
         offsets = keep.tile([P, J // LIST_ROWS], U16, name="offsets")
         raw_words = keep.tile([P, 2, 2 * N], U8, name="raw_words")
         raw_scales = keep.tile([P, 2, N], U8, name="raw_scales")
         planes = [keep.tile([P, T], F32, name="plane%d" % i) for i in range(PACK)]
-        weight = keep.tile([P, J], F32, name="weight")
+        halves = [keep.tile([P, 3, CHUNK], F32, name="half%d" % h) for h in range(2)]
+        weight = [half[:, 0:2, :].rearrange("p c j -> p (c j)") for half in halves]
+        weight_rows = keep.tile([P, P], F32, name="weight_rows")
         wvd_raw = keep.tile([P, PACK, N], F32, name="wvd_raw")
+        identity = keep.tile([P, P], F32, name="identity")
         state = [keep.tile([P, PACK, CHUNK], F32, name="state%d" % c) for c in range(chunks)]
 
         nc.gpsimd.memset(raw_scales[:].rearrange("p w n -> p (w n)").bitcast(I32), 0)
+        make_identity(nc, identity[:])
 
-        def load_scales(w, scales):
+        def load_scales(w, scales, queue):
             for q in range(QUADRANTS):
-                nc.sync.dma_start(
+                queue.dma_start(
                     out=raw_scales[32 * q : 32 * q + 4, w, :].bitcast(I32),
                     in_=scales[0, 4 * q : 4 * q + 4, :].bitcast(I32),
                 )
@@ -78,23 +78,38 @@ def tile_list_dl_sigP_kernel(
         def load_plane(i):
             nc.sync.dma_start(out=planes[i][:], in_=x_rows[:, i, :])
 
-        def load_weight(j0, j1):
-            nc.sync.dma_start(out=weight[:, j0:j1], in_=wgt[:, j0:j1])
-
-        nc.sync.dma_start(offsets[:], offs)
-        load_weight(0, J // 2)
+        nc.sync.dma_start(out=weight_rows[:], in_=wgt.rearrange("(a b) (r c) -> a b r c", b=8, c=P)[:, 0, :, :])
         load_plane(0)
-        load_scales(0, wk_scales)
-        load_weight(J // 2, J)
-        load_plane(1)
+        nc.sync.dma_start(offsets[:], offs)
+        load_scales(0, wk_scales, nc.sync)
+        for i in range(1, PACK):
+            load_plane(i)
         for w, words in enumerate((wk_words, wv4_words)):
             nc.sync.dma_start(out=raw_words[:, w, :].bitcast(I32), in_=words[0].bitcast(I32))
-        load_scales(1, wv4_scales)
-        load_plane(2)
-        load_plane(3)
-        nc.sync.dma_start(out=wvd_raw[:], in_=wvd.rearrange("(p i) n -> p i n", i=PACK))
+        load_scales(1, wv4_scales, nc.sync)
         for c in range(chunks):
             nc.sync.dma_start(out=state[c][:], in_=st_rows[:, :, c * CHUNK : (c + 1) * CHUNK])
+            if c == 0:
+                nc.sync.dma_start(out=wvd_raw[:], in_=wvd.rearrange("(p i) n -> p i n", i=PACK))
+
+        warm = keep.tile([P, 1], F32, name="warm")
+        nc.vector.memset(warm[:], 0.0)
+        warm_out = keep.tile([P, 1], F32, name="warm_out")
+        nc.scalar.activation(out=warm_out[:], in_=warm[:], func=SIGMOID)
+
+        turned = psum.tile([P, BANK], F32, name="ve")
+        nc.tensor.transpose(turned[:, 0:P], weight_rows[:], identity[:])
+        by_block = turned[:, 0:P].rearrange("c (a r) -> c r a", r=8)
+        for c in range(chunks):
+            spread = ring.tile([P, 2, P], F32, name="spread")
+            nc.scalar.copy(
+                out=spread[:].rearrange("c r (a x) -> c r a x", x=8),
+                in_=by_block[:, 2 * c : 2 * c + 2, :].unsqueeze(3).to_broadcast([P, 2, 16, 8]),
+            )
+            bank = psum.tile([P, BANK], F32, name="ke")
+            for r in range(2):
+                nc.tensor.transpose(bank[:, r * P : (r + 1) * P], spread[:, r, :], identity[:])
+            nc.scalar.copy(out=weight[c // 2][:, c % 2 * CHUNK : (c % 2 + 1) * CHUNK], in_=bank[:, 0:CHUNK])
 
         w4_words = keep.tile([P, 2, 2 * N], U8, name="w4_words", align_bytes=64)
         w4_scales = [keep.tile([P, N], U8, name="w4_scales%d" % w, align_bytes=64) for w in range(2)]
@@ -111,44 +126,66 @@ def tile_list_dl_sigP_kernel(
                 in_=raw_scales[:, w, :].rearrange("p (m t) -> p t m", t=PACK),
             )
 
-        picked = keep.tile([P, PACK, J], F32, name="picked")
+        early = keep.tile([P, 2, J], F32, name="early")
+        pairs = [keep.tile([P, 2, CHUNK], F32, name="pair%d" % c)[:] for c in range(2)]
+        pairs.extend(half[:, 0:3:2, :] for half in halves)
 
-        def gather(i, j0, j1):
+        def gather(out, i, j0, j1):
             nc.vector.tensor_tensor(
-                picked[:, i, j0:j1],
+                out,
                 planes[i][:].indirect(offsets[:, j0 // LIST_ROWS : j1 // LIST_ROWS]),
-                weight[:, j0:j1],
+                weight[j0 // BANK][:, j0 % BANK : j0 % BANK + j1 - j0],
                 MULT,
             )
 
-        gather(0, 0, J // 2)
-        deal_scales(0)
-        gather(0, J // 2, J)
-        gather(1, 0, J)
-        deal_words()
-        deal_scales(1)
-        gather(2, 0, J)
-        for c in range(chunks):
-            gather(3, c * CHUNK, (c + 1) * CHUNK)
+        def gather_late(i, c):
+            gather(pairs[c][:, i - 2, :], i, c * CHUNK, (c + 1) * CHUNK)
+
 
         xg_codes = [keep.tile([P, CHUNK], U32, name="xg_codes%d" % c, align_bytes=64) for c in range(chunks)]
         xg_scales = [keep.tile([P, CHUNK], U8, name="xg_scales%d" % c, align_bytes=64) for c in range(chunks)]
 
+        xg_bf = [keep.tile([P, PACK * CHUNK], BF16, name="xg_bf%d" % c, align_bytes=64) for c in range(chunks)]
+
+        def round_picks(c, i, pair):
+            nc.scalar.copy(out=woven(xg_bf[c][:])[:, :, i : i + 2, :], in_=weave(pair))
+
         def quantize_picks(c):
-            xg_bf = ring.tile([P, PACK * CHUNK], BF16, name="xg_bf", align_bytes=64)
-            nc.scalar.copy(out=woven(xg_bf[:]), in_=weave(picked[:, :, c * CHUNK : (c + 1) * CHUNK]))
-            nc.vector.quantize_mx(out=xg_codes[c][:].bitcast(FP8X4), scales=xg_scales[c][:], in_=xg_bf[:])
+            nc.vector.quantize_mx(out=xg_codes[c][:].bitcast(FP8X4), scales=xg_scales[c][:], in_=xg_bf[c][:])
 
         wvd_bf = keep.tile([P, PACK * N], BF16, name="wvd_bf", align_bytes=64)
         wvd_codes = keep.tile([P, N], U32, name="wvd_codes", align_bytes=64)
         wvd_scales = keep.tile([P, N], U8, name="wvd_scales", align_bytes=64)
 
-        def quantize_wvd():
-            nc.vector.tensor_copy(
+        def round_wvd():
+            nc.scalar.copy(
                 out=wvd_bf[:].rearrange("p (u e m i) -> p u m i e", u=2, e=2, i=PACK),
                 in_=wvd_raw[:].rearrange("p i (m u e) -> p u m i e", u=2, e=2),
             )
+
+        def quantize_wvd():
             nc.vector.quantize_mx(out=wvd_codes[:].bitcast(FP8X4), scales=wvd_scales[:], in_=wvd_bf[:])
+
+        for i in range(2):
+            for h in range(2):
+                gather(early[:, i, h * BANK : (h + 1) * BANK], i, h * BANK, (h + 1) * BANK)
+        for c in range(chunks):
+            round_picks(c, 0, early[:, :, c * CHUNK : (c + 1) * CHUNK])
+        gather_late(2, 0)
+        gather_late(2, 1)
+        for c in range(chunks):
+            if c == 2:
+                gather_late(2, c)
+            gather_late(3, c)
+            if c == 3:
+                gather_late(2, c)
+            round_picks(c, 2, pairs[c])
+        deal_words()
+        deal_scales(0)
+        for c in range(chunks):
+            quantize_picks(c)
+        deal_scales(1)
+        round_wvd()
 
         y_codes = keep.tile([P, J], U32, name="y_codes", align_bytes=64)
         y_scales = keep.tile([P, J], U8, name="y_scales", align_bytes=64)
@@ -181,9 +218,9 @@ def tile_list_dl_sigP_kernel(
                 )
             z = ring.tile([P, BANK], F32, name="z")
             nc.vector.tensor_tensor(by_slice(z, ts), ke, state[c][:, ts.start : ts.stop, cs], MULT)
-            gate = ring.tile([P, BANK], F32, name="gate")
-            nc.scalar.activation(out=gate[:], in_=z[:], func=SIGMOID)
-            gates[s] = by_slice(gate, ts)
+            gate = wvd_raw[:, s % PACK, :]
+            nc.scalar.activation(out=gate, in_=z[:], func=SIGMOID)
+            gates[s] = gate.rearrange("p (t j) -> p t j", t=len(ts))
 
         def value_step(s):
             c, ts, cs = part(s)
@@ -231,18 +268,14 @@ def tile_list_dl_sigP_kernel(
             js = slice(c * CHUNK, (c + 1) * CHUNK)
             queue.dma_start(out=out_words[:, js], in_=y_codes[:, js].bitcast(I32))
 
-        quantize_picks(0)
-        quantize_wvd()
-        quantize_picks(1)
         for s in range(LEAD):
             gate_step(s)
+        quantize_wvd()
         for s in range(steps):
             c, h = divmod(s, 2)
-            if s + LEAD < steps:
-                if h == 0 and c + 2 < chunks:
-                    quantize_picks(c + 2)
-                gate_step(s + LEAD)
             value_step(s)
+            if s + LEAD < steps:
+                gate_step(s + LEAD)
             if c == last:
                 round_result(c, h * NARROW, (h + 1) * NARROW, nc.vector.tensor_copy if h == 1 else nc.scalar.copy)
             elif h == 1:

@@ -112,7 +112,7 @@ def tile_list_dl_sigP_kernel(
             nc.scalar.copy(out=weight[c // 2][:, c % 2 * CHUNK : (c % 2 + 1) * CHUNK], in_=bank[:, 0:CHUNK])
 
         w4_words = keep.tile([P, 2, 2 * N], U8, name="w4_words", align_bytes=64)
-        w4_scales = [keep.tile([P, N], U8, name="w4_scales%d" % w, align_bytes=64) for w in range(2)]
+        w4_scales = {0: keep.tile([P, N], U8, name="w4_scales0", align_bytes=64)}
 
         def deal_words():
             nc.vector.tensor_copy(
@@ -120,8 +120,8 @@ def tile_list_dl_sigP_kernel(
                 in_=raw_words[:].bitcast(U16).rearrange("p w (m t) -> p w t m", t=PACK),
             )
 
-        def deal_scales(w):
-            nc.vector.tensor_copy(
+        def deal_scales(w, copy):
+            copy(
                 out=w4_scales[w][:].rearrange("p (t m) -> p t m", t=PACK),
                 in_=raw_scales[:, w, :].rearrange("p (m t) -> p t m", t=PACK),
             )
@@ -181,10 +181,11 @@ def tile_list_dl_sigP_kernel(
                 gather_late(2, c)
             round_picks(c, 2, pairs[c])
         deal_words()
-        deal_scales(0)
+        deal_scales(0, nc.vector.tensor_copy)
         for c in range(chunks):
             quantize_picks(c)
-        deal_scales(1)
+        w4_scales[1] = keep.tile([P, N], U8, name="w4_scales1", tag="xg_bf3", align_bytes=64)
+        deal_scales(1, nc.gpsimd.tensor_copy)
         round_wvd()
 
         y_codes = keep.tile([P, J], U32, name="y_codes", align_bytes=64)
@@ -264,8 +265,8 @@ def tile_list_dl_sigP_kernel(
                 out=y_codes[:, js].bitcast(FP8X4), scales=y_scales[:, js], in_=y_bf[c][:, PACK * lo : PACK * hi]
             )
 
-        def store_codes(c, queue):
-            js = slice(c * CHUNK, (c + 1) * CHUNK)
+        def store_codes(c, lo, hi, queue):
+            js = slice(c * CHUNK + lo, c * CHUNK + hi)
             queue.dma_start(out=out_words[:, js], in_=y_codes[:, js].bitcast(I32))
 
         for s in range(LEAD):
@@ -277,16 +278,27 @@ def tile_list_dl_sigP_kernel(
             if s + LEAD < steps:
                 gate_step(s + LEAD)
             if c == last:
-                round_result(c, h * NARROW, (h + 1) * NARROW, nc.vector.tensor_copy if h == 1 else nc.scalar.copy)
+                if h == 0:
+                    round_result(c, 0, NARROW, nc.scalar.copy)
+            elif h == 1 and c == 0:
+                nc.gpsimd.tensor_scalar(
+                    out=y_bf[c][:].rearrange("p (j t) -> p j t", t=PACK),
+                    in0=y[c][:].rearrange("p t j -> p j t"),
+                    scalar1=1.0,
+                    scalar2=1.0,
+                    op0=MULT,
+                    op1=MULT,
+                )
             elif h == 1:
                 round_result(c, 0, CHUNK, nc.scalar.copy)
-            if h == 0 and c > 0:
+            if c > 0 and h == (0 if c == 2 else 1):
                 quantize_result(c - 1, 0, CHUNK)
-                store_codes(c - 1, nc.sync)
+                store_codes(c - 1, 0, CHUNK, nc.sync)
+        round_result(last, NARROW, CHUNK, nc.vector.tensor_copy)
         quantize_result(last, 0, NARROW)
         quantize_result(last, NARROW, CHUNK)
 
-        store_codes(last, nc.scalar)
+        store_codes(last, 0, CHUNK, nc.scalar)
         for q in range(QUADRANTS):
             queue = nc.sync if q % 2 == 0 else nc.scalar
             queue.dma_start(out=out_scales[4 * q : 4 * q + 4, :], in_=y_scales[32 * q : 32 * q + 4, :].bitcast(I32))

@@ -191,7 +191,7 @@ def tile_list_dl_sigP_kernel(
         y_codes = keep.tile([P, J], U32, name="y_codes", align_bytes=64)
         y_scales = keep.tile([P, J], U8, name="y_scales", align_bytes=64)
         y = [keep.tile([P, PACK, CHUNK], F32, name="y%d" % c) for c in range(chunks)]
-        y_bf = [keep.tile([P, PACK * CHUNK], BF16, name="y_bf%d" % c, align_bytes=64) for c in range(chunks)]
+        y_bf = {c: keep.tile([P, PACK * CHUNK], BF16, name="y_bf%d" % c, align_bytes=64) for c in range(1, chunks)}
         gates = {}
 
         def part(s):
@@ -218,7 +218,12 @@ def tile_list_dl_sigP_kernel(
                     stop=True,
                 )
             z = ring.tile([P, BANK], F32, name="z")
-            nc.vector.tensor_tensor(by_slice(z, ts), ke, state[c][:, ts.start : ts.stop, cs], MULT)
+            if s == steps - 1:
+                keys = keep.tile([P, BANK], F32, name="keys", align_bytes=64)
+                nc.scalar.copy(out=keys[:], in_=ke_bank[:])
+                nc.gpsimd.tensor_tensor(by_slice(z, ts), by_slice(keys, ts), state[c][:, ts.start : ts.stop, cs], MULT)
+            else:
+                nc.vector.tensor_tensor(by_slice(z, ts), ke, state[c][:, ts.start : ts.stop, cs], MULT)
             gate = wvd_raw[:, s % PACK, :]
             nc.scalar.activation(out=gate, in_=z[:], func=SIGMOID)
             gates[s] = gate.rearrange("p (t j) -> p t j", t=len(ts))
@@ -280,20 +285,21 @@ def tile_list_dl_sigP_kernel(
             if c == last:
                 if h == 0:
                     round_result(c, 0, NARROW, nc.scalar.copy)
-            elif h == 1 and c == 0:
+            elif h == 1 and c > 0:
+                round_result(c, 0, CHUNK, nc.scalar.copy)
+            if s + LEAD == steps - 1:
+                y_bf[0] = keep.tile([P, PACK * CHUNK], BF16, name="y_bf0", tag="keys", align_bytes=64)
                 nc.gpsimd.tensor_scalar(
-                    out=y_bf[c][:].rearrange("p (j t) -> p j t", t=PACK),
-                    in0=y[c][:].rearrange("p t j -> p j t"),
+                    out=y_bf[0][:].rearrange("p (j t) -> p j t", t=PACK),
+                    in0=y[0][:].rearrange("p t j -> p j t"),
                     scalar1=1.0,
                     scalar2=1.0,
                     op0=MULT,
                     op1=MULT,
                 )
-            elif h == 1:
-                round_result(c, 0, CHUNK, nc.scalar.copy)
-            if c > 0 and h == (0 if c == 2 else 1):
-                quantize_result(c - 1, 0, CHUNK)
-                store_codes(c - 1, 0, CHUNK, nc.sync)
+            if s >= steps - last:
+                quantize_result(s - steps + last, 0, CHUNK)
+                store_codes(s - steps + last, 0, CHUNK, nc.sync)
         round_result(last, NARROW, CHUNK, nc.vector.tensor_copy)
         quantize_result(last, 0, NARROW)
         quantize_result(last, NARROW, CHUNK)

@@ -26,6 +26,8 @@ CHUNK = 256
 NARROW = 128
 DEPTH = 4
 LEAD = 4
+BLOCKS = J // P
+REPEAT = 8
 
 
 def weave(rows):
@@ -58,8 +60,9 @@ def tile_list_dl_sigP_kernel(
         raw_words = keep.tile([P, 2, 2 * N], U8, name="raw_words")
         raw_scales = keep.tile([P, 2, N], U8, name="raw_scales")
         planes = [keep.tile([P, T], F32, name="plane%d" % i) for i in range(PACK)]
-        halves = [keep.tile([P, 3, CHUNK], F32, name="half%d" % h) for h in range(2)]
-        weight = [half[:, 0:2, :].rearrange("p c j -> p (c j)") for half in halves]
+        first_half = keep.tile([P, BANK], F32, name="first_half")
+        second_half = keep.tile([P, 3, CHUNK], F32, name="second_half")
+        weight = [first_half[:], second_half[:, 0:2, :].rearrange("p c j -> p (c j)")]
         weight_rows = keep.tile([P, P], F32, name="weight_rows")
         wvd_raw = keep.tile([P, PACK, N], F32, name="wvd_raw")
         identity = keep.tile([P, P], F32, name="identity")
@@ -68,9 +71,9 @@ def tile_list_dl_sigP_kernel(
         nc.gpsimd.memset(raw_scales[:].rearrange("p w n -> p (w n)").bitcast(I32), 0)
         make_identity(nc, identity[:])
 
-        def load_scales(w, scales, queue):
+        def load_scales(w, scales):
             for q in range(QUADRANTS):
-                queue.dma_start(
+                nc.sync.dma_start(
                     out=raw_scales[32 * q : 32 * q + 4, w, :].bitcast(I32),
                     in_=scales[0, 4 * q : 4 * q + 4, :].bitcast(I32),
                 )
@@ -78,15 +81,15 @@ def tile_list_dl_sigP_kernel(
         def load_plane(i):
             nc.sync.dma_start(out=planes[i][:], in_=x_rows[:, i, :])
 
-        nc.sync.dma_start(out=weight_rows[:], in_=wgt.rearrange("(a b) (r c) -> a b r c", b=8, c=P)[:, 0, :, :])
+        nc.sync.dma_start(out=weight_rows[:], in_=wgt.rearrange("(a b) (r c) -> a b r c", b=REPEAT, c=P)[:, 0, :, :])
         load_plane(0)
         nc.sync.dma_start(offsets[:], offs)
-        load_scales(0, wk_scales, nc.sync)
+        load_scales(0, wk_scales)
         for i in range(1, PACK):
             load_plane(i)
         for w, words in enumerate((wk_words, wv4_words)):
             nc.sync.dma_start(out=raw_words[:, w, :].bitcast(I32), in_=words[0].bitcast(I32))
-        load_scales(1, wv4_scales, nc.sync)
+        load_scales(1, wv4_scales)
         for c in range(chunks):
             nc.sync.dma_start(out=state[c][:], in_=st_rows[:, :, c * CHUNK : (c + 1) * CHUNK])
             if c == 0:
@@ -97,19 +100,19 @@ def tile_list_dl_sigP_kernel(
         warm_out = keep.tile([P, 1], F32, name="warm_out")
         nc.scalar.activation(out=warm_out[:], in_=warm[:], func=SIGMOID)
 
-        turned = psum.tile([P, BANK], F32, name="ve")
+        turned = psum.tile([P, BANK], F32, name="turned", tag="ve")
         nc.tensor.transpose(turned[:, 0:P], weight_rows[:], identity[:])
-        by_block = turned[:, 0:P].rearrange("c (a r) -> c r a", r=8)
+        by_block = turned[:, 0:P].rearrange("c (a r) -> c r a", r=BLOCKS)
         for c in range(chunks):
             spread = ring.tile([P, 2, P], F32, name="spread")
             nc.scalar.copy(
-                out=spread[:].rearrange("c r (a x) -> c r a x", x=8),
-                in_=by_block[:, 2 * c : 2 * c + 2, :].unsqueeze(3).to_broadcast([P, 2, 16, 8]),
+                out=spread[:].rearrange("c r (a x) -> c r a x", x=REPEAT),
+                in_=by_block[:, 2 * c : 2 * c + 2, :].unsqueeze(3).to_broadcast([P, 2, P // REPEAT, REPEAT]),
             )
-            bank = psum.tile([P, BANK], F32, name="ke")
+            turned_back = psum.tile([P, BANK], F32, name="turned_back", tag="ke")
             for r in range(2):
-                nc.tensor.transpose(bank[:, r * P : (r + 1) * P], spread[:, r, :], identity[:])
-            nc.scalar.copy(out=weight[c // 2][:, c % 2 * CHUNK : (c % 2 + 1) * CHUNK], in_=bank[:, 0:CHUNK])
+                nc.tensor.transpose(turned_back[:, r * P : (r + 1) * P], spread[:, r, :], identity[:])
+            nc.scalar.copy(out=weight[c // 2][:, c % 2 * CHUNK : (c % 2 + 1) * CHUNK], in_=turned_back[:, 0:CHUNK])
 
         w4_words = keep.tile([P, 2, 2 * N], U8, name="w4_words", align_bytes=64)
         w4_scales = {0: keep.tile([P, N], U8, name="w4_scales0", align_bytes=64)}
@@ -127,8 +130,8 @@ def tile_list_dl_sigP_kernel(
             )
 
         early = keep.tile([P, 2, J], F32, name="early")
-        pairs = [keep.tile([P, 2, CHUNK], F32, name="pair%d" % c)[:] for c in range(2)]
-        pairs.extend(half[:, 0:3:2, :] for half in halves)
+        pairs = [keep.tile([P, 2, CHUNK], F32, name="pair%d" % c)[:] for c in range(last)]
+        pairs.append(second_half[:, 0:3:2, :])
 
         def gather(out, i, j0, j1):
             nc.vector.tensor_tensor(
@@ -141,10 +144,8 @@ def tile_list_dl_sigP_kernel(
         def gather_late(i, c):
             gather(pairs[c][:, i - 2, :], i, c * CHUNK, (c + 1) * CHUNK)
 
-
         xg_codes = [keep.tile([P, CHUNK], U32, name="xg_codes%d" % c, align_bytes=64) for c in range(chunks)]
         xg_scales = [keep.tile([P, CHUNK], U8, name="xg_scales%d" % c, align_bytes=64) for c in range(chunks)]
-
         xg_bf = [keep.tile([P, PACK * CHUNK], BF16, name="xg_bf%d" % c, align_bytes=64) for c in range(chunks)]
 
         def round_picks(c, i, pair):
@@ -171,20 +172,18 @@ def tile_list_dl_sigP_kernel(
                 gather(early[:, i, h * BANK : (h + 1) * BANK], i, h * BANK, (h + 1) * BANK)
         for c in range(chunks):
             round_picks(c, 0, early[:, :, c * CHUNK : (c + 1) * CHUNK])
-        gather_late(2, 0)
-        gather_late(2, 1)
+        for c in range(last):
+            gather_late(2, c)
         for c in range(chunks):
-            if c == 2:
-                gather_late(2, c)
             gather_late(3, c)
-            if c == 3:
+            if c == last:
                 gather_late(2, c)
             round_picks(c, 2, pairs[c])
         deal_words()
         deal_scales(0, nc.vector.tensor_copy)
         for c in range(chunks):
             quantize_picks(c)
-        w4_scales[1] = keep.tile([P, N], U8, name="w4_scales1", tag="xg_bf3", align_bytes=64)
+        w4_scales[1] = keep.tile([P, N], U8, name="w4_scales1", tag="xg_bf%d" % last, align_bytes=64)
         deal_scales(1, nc.gpsimd.tensor_copy)
         round_wvd()
 
@@ -270,8 +269,8 @@ def tile_list_dl_sigP_kernel(
                 out=y_codes[:, js].bitcast(FP8X4), scales=y_scales[:, js], in_=y_bf[c][:, PACK * lo : PACK * hi]
             )
 
-        def store_codes(c, lo, hi, queue):
-            js = slice(c * CHUNK + lo, c * CHUNK + hi)
+        def store_codes(c, queue):
+            js = slice(c * CHUNK, (c + 1) * CHUNK)
             queue.dma_start(out=out_words[:, js], in_=y_codes[:, js].bitcast(I32))
 
         for s in range(LEAD):
@@ -282,10 +281,9 @@ def tile_list_dl_sigP_kernel(
             value_step(s)
             if s + LEAD < steps:
                 gate_step(s + LEAD)
-            if c == last:
-                if h == 0:
-                    round_result(c, 0, NARROW, nc.scalar.copy)
-            elif h == 1 and c > 0:
+            if c == last and h == 0:
+                round_result(c, 0, NARROW, nc.scalar.copy)
+            if 0 < c < last and h == 1:
                 round_result(c, 0, CHUNK, nc.scalar.copy)
             if s + LEAD == steps - 1:
                 y_bf[0] = keep.tile([P, PACK * CHUNK], BF16, name="y_bf0", tag="keys", align_bytes=64)
@@ -299,12 +297,12 @@ def tile_list_dl_sigP_kernel(
                 )
             if s >= steps - last:
                 quantize_result(s - steps + last, 0, CHUNK)
-                store_codes(s - steps + last, 0, CHUNK, nc.sync)
+                store_codes(s - steps + last, nc.sync)
         round_result(last, NARROW, CHUNK, nc.vector.tensor_copy)
         quantize_result(last, 0, NARROW)
         quantize_result(last, NARROW, CHUNK)
 
-        store_codes(last, 0, CHUNK, nc.scalar)
+        store_codes(last, nc.scalar)
         for q in range(QUADRANTS):
             queue = nc.sync if q % 2 == 0 else nc.scalar
             queue.dma_start(out=out_scales[4 * q : 4 * q + 4, :], in_=y_scales[32 * q : 32 * q + 4, :].bitcast(I32))

@@ -24,6 +24,7 @@ LIST_ROWS = 16
 BANK = 512
 CHUNK = 256
 NARROW = 128
+HALF = CHUNK // 2
 DEPTH = 4
 LEAD = 4
 BLOCKS = J // P
@@ -31,11 +32,11 @@ REPEAT = 8
 
 
 def weave(rows):
-    return rows.rearrange("p t (c e) -> p c t e", e=2)
+    return rows.rearrange("p t (pair e) -> p pair t e", e=2)
 
 
 def woven(packed):
-    return packed.rearrange("p (c e t) -> p c t e", e=2, t=PACK)
+    return packed.rearrange("p (pair e t) -> p pair t e", e=2, t=PACK)
 
 
 def tile_list_dl_sigP_kernel(
@@ -45,7 +46,7 @@ def tile_list_dl_sigP_kernel(
     chunks = J // CHUNK
     steps = 2 * chunks
     last = chunks - 1
-    x_rows = xT.rearrange("(p i) t -> p i t", i=PACK)
+    x_rows = xT.rearrange("(p i) token -> p i token", i=PACK)
     st_rows = st.rearrange("(p t) j -> p t j", t=PACK)
     out_rows = out_0.rearrange("(p t) j -> p t j", t=PACK)
     out_words = out_1[0].rearrange("p j i -> p (j i)").bitcast(I32)
@@ -81,7 +82,7 @@ def tile_list_dl_sigP_kernel(
         def load_plane(i):
             nc.sync.dma_start(out=planes[i][:], in_=x_rows[:, i, :])
 
-        nc.sync.dma_start(out=weight_rows[:], in_=wgt.rearrange("(a b) (r c) -> a b r c", b=REPEAT, c=P)[:, 0, :, :])
+        nc.sync.dma_start(out=weight_rows[:], in_=wgt.rearrange("(a b) (r j) -> a b r j", b=REPEAT, j=P)[:, 0, :, :])
         load_plane(0)
         nc.sync.dma_start(offsets[:], offs)
         load_scales(0, wk_scales)
@@ -102,11 +103,11 @@ def tile_list_dl_sigP_kernel(
 
         turned = psum.tile([P, BANK], F32, name="turned", tag="ve")
         nc.tensor.transpose(turned[:, 0:P], weight_rows[:], identity[:])
-        by_block = turned[:, 0:P].rearrange("c (a r) -> c r a", r=BLOCKS)
+        by_block = turned[:, 0:P].rearrange("j (a r) -> j r a", r=BLOCKS)
         for c in range(chunks):
             spread = ring.tile([P, 2, P], F32, name="spread")
             nc.scalar.copy(
-                out=spread[:].rearrange("c r (a x) -> c r a x", x=REPEAT),
+                out=spread[:].rearrange("j r (a x) -> j r a x", x=REPEAT),
                 in_=by_block[:, 2 * c : 2 * c + 2, :].unsqueeze(3).to_broadcast([P, 2, P // REPEAT, REPEAT]),
             )
             turned_back = psum.tile([P, BANK], F32, name="turned_back", tag="ke")
@@ -160,16 +161,16 @@ def tile_list_dl_sigP_kernel(
 
         def round_wvd():
             nc.scalar.copy(
-                out=wvd_bf[:].rearrange("p (u e m i) -> p u m i e", u=2, e=2, i=PACK),
-                in_=wvd_raw[:].rearrange("p i (m u e) -> p u m i e", u=2, e=2),
+                out=wvd_bf[:].rearrange("p (h u m i) -> p h m i u", h=2, u=2, i=PACK),
+                in_=wvd_raw[:].rearrange("p i (m h u) -> p h m i u", h=2, u=2),
             )
 
         def quantize_wvd():
             nc.vector.quantize_mx(out=wvd_codes[:].bitcast(FP8X4), scales=wvd_scales[:], in_=wvd_bf[:])
 
         for i in range(2):
-            for h in range(2):
-                gather(early[:, i, h * BANK : (h + 1) * BANK], i, h * BANK, (h + 1) * BANK)
+            for j0 in range(0, J, BANK):
+                gather(early[:, i, j0 : j0 + BANK], i, j0, j0 + BANK)
         for c in range(chunks):
             round_picks(c, 0, early[:, :, c * CHUNK : (c + 1) * CHUNK])
         for c in range(last):
@@ -193,51 +194,46 @@ def tile_list_dl_sigP_kernel(
         y_bf = {c: keep.tile([P, PACK * CHUNK], BF16, name="y_bf%d" % c, align_bytes=64) for c in range(1, chunks)}
         gates = {}
 
-        def part(s):
-            c, h = divmod(s, 2)
-            if c == last:
-                return c, range(PACK), slice(h * NARROW, (h + 1) * NARROW)
-            return c, range(2 * h, 2 * h + 2), slice(0, CHUNK)
-
-        def by_slice(tile, ts):
-            return tile[:].rearrange("p (t j) -> p t j", t=len(ts))
+        def by_slice(bank):
+            return bank.rearrange("p (u j) -> p u j", u=2)
 
         def gate_step(s):
-            c, ts, cs = part(s)
-            ke_bank = psum.tile([P, BANK], F32, name="ke")
-            ke = by_slice(ke_bank, ts)
-            for t in ts:
+            c, h = divmod(s, 2)
+            ke = psum.tile([P, BANK], F32, name="ke")
+            for u in range(2):
+                t = 2 * h + u
                 nc.tensor.matmul_mx(
-                    out=ke[:, t - ts.start, :],
+                    out=by_slice(ke[:])[:, u, :],
                     lhsT=w4_words[:, 0, 2 * P * t : 2 * P * (t + 1)].bitcast(FP4X4),
                     lhsT_scale=w4_scales[0][:, P * t : P * (t + 1)],
-                    rhs=xg_codes[c][:, cs].bitcast(FP8X4),
-                    rhs_scale=xg_scales[c][:, cs],
+                    rhs=xg_codes[c][:].bitcast(FP8X4),
+                    rhs_scale=xg_scales[c][:],
                     start=True,
                     stop=True,
                 )
             z = ring.tile([P, BANK], F32, name="z")
+            st_part = state[c][:, 2 * h : 2 * h + 2, :]
             if s == steps - 1:
                 keys = keep.tile([P, BANK], F32, name="keys", align_bytes=64)
-                nc.scalar.copy(out=keys[:], in_=ke_bank[:])
-                nc.gpsimd.tensor_tensor(by_slice(z, ts), by_slice(keys, ts), state[c][:, ts.start : ts.stop, cs], MULT)
+                nc.scalar.copy(out=keys[:], in_=ke[:])
+                nc.gpsimd.tensor_tensor(by_slice(z[:]), by_slice(keys[:]), st_part, MULT)
             else:
-                nc.vector.tensor_tensor(by_slice(z, ts), ke, state[c][:, ts.start : ts.stop, cs], MULT)
+                nc.vector.tensor_tensor(by_slice(z[:]), by_slice(ke[:]), st_part, MULT)
             gate = wvd_raw[:, s % PACK, :]
             nc.scalar.activation(out=gate, in_=z[:], func=SIGMOID)
-            gates[s] = gate.rearrange("p (t j) -> p t j", t=len(ts))
+            gates[s] = by_slice(gate)
 
         def value_step(s):
-            c, ts, cs = part(s)
-            ve_bank = psum.tile([P, BANK], F32, name="ve")
-            ve = by_slice(ve_bank, ts)
-            for t in ts:
-                for j0 in range(cs.start, cs.stop, NARROW):
+            c, h = divmod(s, 2)
+            ve_bank = psum.tile([P, BANK], F32, name="ve_bank", tag="ve")
+            ve = by_slice(ve_bank[:])
+            for u in range(2):
+                t = 2 * h + u
+                for j0 in range(0, CHUNK, NARROW):
                     js = slice(j0, j0 + NARROW)
-                    acc = ve[:, t - ts.start, j0 - cs.start : j0 - cs.start + NARROW]
                     rhs, rhs_scale = xg_codes[c][:, js].bitcast(FP8X4), xg_scales[c][:, js]
                     nc.tensor.matmul_mx(
-                        out=acc,
+                        out=ve[:, u, js],
                         lhsT=w4_words[:, 1, 2 * P * t : 2 * P * (t + 1)].bitcast(FP4X4),
                         lhsT_scale=w4_scales[1][:, P * t : P * (t + 1)],
                         rhs=rhs,
@@ -246,7 +242,7 @@ def tile_list_dl_sigP_kernel(
                         stop=False,
                     )
                     nc.tensor.matmul_mx(
-                        out=acc,
+                        out=ve[:, u, js],
                         lhsT=wvd_codes[:, P * t : P * (t + 1)].bitcast(FP8X4),
                         lhsT_scale=wvd_scales[:, P * t : P * (t + 1)],
                         rhs=rhs,
@@ -254,11 +250,9 @@ def tile_list_dl_sigP_kernel(
                         start=False,
                         stop=True,
                     )
-            result = y[c][:, ts.start : ts.stop, cs]
+            result = y[c][:, 2 * h : 2 * h + 2, :]
             nc.vector.tensor_tensor(result, ve, gates[s], MULT)
-            nc.sync.dma_start(
-                out=out_rows[:, ts.start : ts.stop, c * CHUNK + cs.start : c * CHUNK + cs.stop], in_=result
-            )
+            nc.sync.dma_start(out=out_rows[:, 2 * h : 2 * h + 2, c * CHUNK : (c + 1) * CHUNK], in_=result)
 
         def round_result(c, lo, hi, copy):
             copy(out=woven(y_bf[c][:, PACK * lo : PACK * hi]), in_=weave(y[c][:, :, lo:hi]))
@@ -281,10 +275,8 @@ def tile_list_dl_sigP_kernel(
             value_step(s)
             if s + LEAD < steps:
                 gate_step(s + LEAD)
-            if c == last and h == 0:
-                round_result(c, 0, NARROW, nc.scalar.copy)
-            if 0 < c < last and h == 1:
-                round_result(c, 0, CHUNK, nc.scalar.copy)
+            if c > 0 and h == 1:
+                round_result(c, 0, HALF if c == last else CHUNK, nc.scalar.copy)
             if s + LEAD == steps - 1:
                 y_bf[0] = keep.tile([P, PACK * CHUNK], BF16, name="y_bf0", tag="keys", align_bytes=64)
                 nc.gpsimd.tensor_scalar(
@@ -298,9 +290,9 @@ def tile_list_dl_sigP_kernel(
             if s >= steps - last:
                 quantize_result(s - steps + last, 0, CHUNK)
                 store_codes(s - steps + last, nc.sync)
-        round_result(last, NARROW, CHUNK, nc.vector.tensor_copy)
-        quantize_result(last, 0, NARROW)
-        quantize_result(last, NARROW, CHUNK)
+        round_result(last, HALF, CHUNK, nc.vector.tensor_copy)
+        quantize_result(last, HALF, CHUNK)
+        quantize_result(last, 0, HALF)
 
         store_codes(last, nc.scalar)
         for q in range(QUADRANTS):

@@ -263,8 +263,8 @@ def tile_list_dl_sigP_kernel(
                 out=y_codes[:, js].bitcast(FP8X4), scales=y_scales[:, js], in_=y_bf[c][:, PACK * lo : PACK * hi]
             )
 
-        def store_codes(c, queue):
-            js = slice(c * CHUNK, (c + 1) * CHUNK)
+        def store_codes(c0, c1, queue):
+            js = slice(c0 * CHUNK, c1 * CHUNK)
             queue.dma_start(out=out_words[:, js], in_=y_codes[:, js].bitcast(I32))
 
         for s in range(LEAD):
@@ -287,14 +287,17 @@ def tile_list_dl_sigP_kernel(
                     op0=MULT,
                     op1=MULT,
                 )
-            if s >= steps - last:
-                quantize_result(s - steps + last, 0, CHUNK)
-                store_codes(s - steps + last, nc.sync)
+            if s == steps - 2:
+                quantize_result(0, 0, CHUNK)
+                quantize_result(1, 0, CHUNK)
+                store_codes(0, 2, nc.sync)
+        quantize_result(last - 1, 0, CHUNK)
+        store_codes(last - 1, last, nc.sync)
         round_result(last, HALF, CHUNK, nc.vector.tensor_copy)
         quantize_result(last, HALF, CHUNK)
         quantize_result(last, 0, HALF)
 
-        store_codes(last, nc.scalar)
+        store_codes(last, chunks, nc.scalar)
         for q in range(QUADRANTS):
             queue = nc.sync if q % 2 == 0 else nc.scalar
             queue.dma_start(out=out_scales[4 * q : 4 * q + 4, :], in_=y_scales[32 * q : 32 * q + 4, :].bitcast(I32))

@@ -86,10 +86,11 @@ def tile_list_dl_sigP_kernel(
         load_plane(0)
         nc.sync.dma_start(offsets[:], offs)
         load_scales(0, wk_scales)
-        for i in range(1, PACK):
-            load_plane(i)
+        load_plane(1)
         for w, words in enumerate((wk_words, wv4_words)):
             nc.sync.dma_start(out=raw_words[:, w, :].bitcast(I32), in_=words[0].bitcast(I32))
+        for i in range(2, PACK):
+            load_plane(i)
         load_scales(1, wv4_scales)
         for c in range(chunks):
             nc.sync.dma_start(out=state[c][:], in_=st_rows[:, :, c * CHUNK : (c + 1) * CHUNK])
@@ -119,7 +120,7 @@ def tile_list_dl_sigP_kernel(
         w4_scales = {0: keep.tile([P, N], U8, name="w4_scales0", align_bytes=64)}
 
         def deal_words():
-            nc.vector.tensor_copy(
+            nc.scalar.copy(
                 out=w4_words[:].bitcast(U16).rearrange("p w (t m) -> p w t m", t=PACK),
                 in_=raw_words[:].bitcast(U16).rearrange("p w (m t) -> p w t m", t=PACK),
             )
@@ -168,6 +169,7 @@ def tile_list_dl_sigP_kernel(
         def quantize_wvd():
             nc.vector.quantize_mx(out=wvd_codes[:].bitcast(FP8X4), scales=wvd_scales[:], in_=wvd_bf[:])
 
+        deal_words()
         for i in range(2):
             for j0 in range(0, J, BANK):
                 gather(early[:, i, j0 : j0 + BANK], i, j0, j0 + BANK)
@@ -180,7 +182,6 @@ def tile_list_dl_sigP_kernel(
             if c == last:
                 gather_late(2, c)
             round_picks(c, 2, pairs[c])
-        deal_words()
         deal_scales(0, nc.vector.tensor_copy)
         for c in range(chunks):
             quantize_picks(c)

@@ -67,7 +67,7 @@ def tile_list_dl_sigP_kernel(
         weight_rows = keep.tile([P, P], F32, name="weight_rows")
         wvd_raw = keep.tile([P, PACK, N], F32, name="wvd_raw")
         identity = keep.tile([P, P], F32, name="identity")
-        state = [keep.tile([P, PACK, CHUNK], F32, name="state%d" % c) for c in range(chunks)]
+        state = [keep.tile([P, PACK, CHUNK], F32, name="state%d" % c, align_bytes=64) for c in range(chunks)]
 
         nc.gpsimd.memset(raw_scales[:].rearrange("p w n -> p (w n)").bitcast(I32), 0)
         make_identity(nc, identity[:])
@@ -91,10 +91,10 @@ def tile_list_dl_sigP_kernel(
             nc.sync.dma_start(out=raw_words[:, w, :].bitcast(I32), in_=words[0].bitcast(I32))
         for i in range(2, PACK):
             load_plane(i)
-        load_scales(1, wv4_scales)
         for c in range(chunks):
             nc.sync.dma_start(out=state[c][:], in_=st_rows[:, :, c * CHUNK : (c + 1) * CHUNK])
             if c == 0:
+                load_scales(1, wv4_scales)
                 nc.sync.dma_start(out=wvd_raw[:], in_=wvd.rearrange("(p i) n -> p i n", i=PACK))
 
         warm = keep.tile([P, 1], F32, name="warm")
@@ -183,28 +183,33 @@ def tile_list_dl_sigP_kernel(
                 gather_late(2, c)
             round_picks(c, 2, pairs[c])
         deal_scales(0, nc.vector.tensor_copy)
-        for c in range(chunks):
+        for c in range(last):
             quantize_picks(c)
-        w4_scales[1] = keep.tile([P, N], U8, name="w4_scales1", tag="xg_bf%d" % last, align_bytes=64)
-        deal_scales(1, nc.gpsimd.tensor_copy)
         round_wvd()
 
-        y_codes = keep.tile([P, J], U32, name="y_codes", align_bytes=64)
         y_scales = keep.tile([P, J], U8, name="y_scales", align_bytes=64)
         y = [keep.tile([P, PACK, CHUNK], F32, name="y%d" % c) for c in range(chunks)]
         y_bf = {c: keep.tile([P, PACK * CHUNK], BF16, name="y_bf%d" % c, align_bytes=64) for c in range(1, chunks)}
-        gates = {}
+        y_codes = {c: keep.tile([P, CHUNK], U32, name="y_codes%d" % c, align_bytes=64)[:] for c in range(2, chunks)}
+        z = {s: keep.tile([P, BANK], F32, name="z%d" % s, align_bytes=64)[:] for s in range(steps - 2)}
+        gates = {s: z[s - 2] for s in range(2, steps)}
+        gates[0], gates[1] = wvd_raw[:, 2, :], wvd_raw[:, 3, :]
+        ke = {}
 
         def by_slice(bank):
             return bank.rearrange("p (u j) -> p u j", u=2)
 
-        def gate_step(s):
+        def st_part(s):
             c, h = divmod(s, 2)
-            ke = psum.tile([P, BANK], F32, name="ke")
+            return state[c][:, 2 * h : 2 * h + 2, :]
+
+        def key_matmuls(s):
+            c, h = divmod(s, 2)
+            ke[s] = psum.tile([P, BANK], F32, name="ke")
             for u in range(2):
                 t = 2 * h + u
                 nc.tensor.matmul_mx(
-                    out=by_slice(ke[:])[:, u, :],
+                    out=by_slice(ke[s][:])[:, u, :],
                     lhsT=w4_words[:, 0, 2 * P * t : 2 * P * (t + 1)].bitcast(FP4X4),
                     lhsT_scale=w4_scales[0][:, P * t : P * (t + 1)],
                     rhs=xg_codes[c][:].bitcast(FP8X4),
@@ -212,17 +217,19 @@ def tile_list_dl_sigP_kernel(
                     start=True,
                     stop=True,
                 )
-            z = ring.tile([P, BANK], F32, name="z")
-            st_part = state[c][:, 2 * h : 2 * h + 2, :]
-            if s == steps - 1:
-                keys = keep.tile([P, BANK], F32, name="keys", align_bytes=64)
-                nc.scalar.copy(out=keys[:], in_=ke[:])
-                nc.gpsimd.tensor_tensor(by_slice(z[:]), by_slice(keys[:]), st_part, MULT)
-            else:
-                nc.vector.tensor_tensor(by_slice(z[:]), by_slice(ke[:]), st_part, MULT)
-            gate = wvd_raw[:, s % PACK, :]
-            nc.scalar.activation(out=gate, in_=z[:], func=SIGMOID)
-            gates[s] = by_slice(gate)
+
+        def key_product(s):
+            key_matmuls(s)
+            nc.vector.tensor_tensor(by_slice(z[s]), by_slice(ke[s][:]), st_part(s), MULT)
+
+        def key_product_aside(s):
+            key_matmuls(s)
+            keys = wvd_raw[:, s % 2, :]
+            nc.scalar.copy(out=keys, in_=ke[s][:])
+            nc.gpsimd.tensor_tensor(by_slice(z[s]), by_slice(keys), st_part(s), MULT)
+
+        def sigmoid(s):
+            nc.scalar.activation(out=gates[s], in_=z[s], func=SIGMOID)
 
         def value_step(s):
             c, h = divmod(s, 2)
@@ -252,53 +259,58 @@ def tile_list_dl_sigP_kernel(
                         stop=True,
                     )
             result = y[c][:, 2 * h : 2 * h + 2, :]
-            nc.vector.tensor_tensor(result, ve, gates[s], MULT)
+            nc.vector.tensor_tensor(result, ve, by_slice(gates[s]), MULT)
             nc.sync.dma_start(out=out_rows[:, 2 * h : 2 * h + 2, c * CHUNK : (c + 1) * CHUNK], in_=result)
 
         def round_result(c, lo, hi, copy):
             copy(out=woven(y_bf[c][:, PACK * lo : PACK * hi]), in_=weave(y[c][:, :, lo:hi]))
 
+        def round_result_aside(c):
+            nc.gpsimd.tensor_copy(
+                out=y_bf[c][:].rearrange("p (j t) -> p j t", t=PACK), in_=y[c][:].rearrange("p t j -> p j t")
+            )
+
         def quantize_result(c, lo, hi):
             js = slice(c * CHUNK + lo, c * CHUNK + hi)
             nc.vector.quantize_mx(
-                out=y_codes[:, js].bitcast(FP8X4), scales=y_scales[:, js], in_=y_bf[c][:, PACK * lo : PACK * hi]
+                out=y_codes[c][:, lo:hi].bitcast(FP8X4), scales=y_scales[:, js], in_=y_bf[c][:, PACK * lo : PACK * hi]
             )
 
-        def store_codes(c0, c1, queue):
-            js = slice(c0 * CHUNK, c1 * CHUNK)
-            queue.dma_start(out=out_words[:, js], in_=y_codes[:, js].bitcast(I32))
-
-        for s in range(LEAD):
-            gate_step(s)
+        key_product(0)
+        quantize_picks(last)
+        w4_scales[1] = keep.tile([P, N], U8, name="w4_scales1", tag="xg_bf%d" % last, align_bytes=64)
+        deal_scales(1, nc.gpsimd.tensor_copy)
+        for s in range(1, LEAD):
+            key_product(s)
         quantize_wvd()
+        z_aside = keep.tile([P, 2, BANK], F32, name="z_aside", tag="wvd_bf", align_bytes=64)
+        z[steps - 2], z[steps - 1] = z_aside[:, 0, :], z_aside[:, 1, :]
+        for s in range(steps - 2, steps):
+            key_product_aside(s)
+        for s in range(LEAD, steps - 2):
+            key_product(s)
+        for s in range(steps):
+            sigmoid(s)
+        y_bf[0] = keep.tile([P, PACK * CHUNK], BF16, name="y_bf0", tag="state%d" % last, align_bytes=64)
         for s in range(steps):
             c, h = divmod(s, 2)
             value_step(s)
-            if s + LEAD < steps:
-                gate_step(s + LEAD)
-            if c > 0 and h == 1:
+            if h == 1 and c < 2:
+                round_result_aside(c)
+            elif h == 1:
                 round_result(c, 0, HALF if c == last else CHUNK, nc.scalar.copy)
-            if s + LEAD == steps - 1:
-                y_bf[0] = keep.tile([P, PACK * CHUNK], BF16, name="y_bf0", tag="keys", align_bytes=64)
-                nc.gpsimd.tensor_scalar(
-                    out=y_bf[0][:].rearrange("p (j t) -> p j t", t=PACK),
-                    in0=y[0][:].rearrange("p t j -> p j t"),
-                    scalar1=1.0,
-                    scalar2=1.0,
-                    op0=MULT,
-                    op1=MULT,
-                )
-            if s == steps - 2:
-                quantize_result(0, 0, CHUNK)
-                quantize_result(1, 0, CHUNK)
-                store_codes(0, 2, nc.sync)
-        quantize_result(last - 1, 0, CHUNK)
-        store_codes(last - 1, last, nc.sync)
+        first_codes = keep.tile([P, 2 * CHUNK], U32, name="first_codes", tag="z%d" % (steps - 3), align_bytes=64)
+        for c in range(2):
+            y_codes[c] = first_codes[:, c * CHUNK : (c + 1) * CHUNK]
+            quantize_result(c, 0, CHUNK)
+        nc.sync.dma_start(out=out_words[:, 0 : 2 * CHUNK], in_=first_codes[:].bitcast(I32))
         round_result(last, HALF, CHUNK, nc.vector.tensor_copy)
+        quantize_result(2, 0, CHUNK)
+        nc.sync.dma_start(out=out_words[:, 2 * CHUNK : 3 * CHUNK], in_=y_codes[2].bitcast(I32))
         quantize_result(last, HALF, CHUNK)
         quantize_result(last, 0, HALF)
 
-        store_codes(last, chunks, nc.scalar)
+        nc.scalar.dma_start(out=out_words[:, last * CHUNK : J], in_=y_codes[last].bitcast(I32))
         for q in range(QUADRANTS):
             queue = nc.sync if q % 2 == 0 else nc.scalar
             queue.dma_start(out=out_scales[4 * q : 4 * q + 4, :], in_=y_scales[32 * q : 32 * q + 4, :].bitcast(I32))

@@ -91,10 +91,10 @@ def tile_list_dl_sigP_kernel(
             nc.sync.dma_start(out=raw_words[:, w, :].bitcast(I32), in_=words[0].bitcast(I32))
         for i in range(2, PACK):
             load_plane(i)
+        load_scales(1, wv4_scales)
         for c in range(chunks):
             nc.sync.dma_start(out=state[c][:], in_=st_rows[:, :, c * CHUNK : (c + 1) * CHUNK])
             if c == 0:
-                load_scales(1, wv4_scales)
                 nc.sync.dma_start(out=wvd_raw[:], in_=wvd.rearrange("(p i) n -> p i n", i=PACK))
 
         warm = keep.tile([P, 1], F32, name="warm")
@@ -265,9 +265,10 @@ def tile_list_dl_sigP_kernel(
         def round_result(c, lo, hi, copy):
             copy(out=woven(y_bf[c][:, PACK * lo : PACK * hi]), in_=weave(y[c][:, :, lo:hi]))
 
-        def round_result_aside(c):
+        def round_result_aside(c, hi):
             nc.gpsimd.tensor_copy(
-                out=y_bf[c][:].rearrange("p (j t) -> p j t", t=PACK), in_=y[c][:].rearrange("p t j -> p j t")
+                out=y_bf[c][:, 0 : PACK * hi].rearrange("p (j t) -> p j t", t=PACK),
+                in_=y[c][:, :, 0:hi].rearrange("p t j -> p j t"),
             )
 
         def quantize_result(c, lo, hi):
@@ -276,11 +277,10 @@ def tile_list_dl_sigP_kernel(
                 out=y_codes[c][:, lo:hi].bitcast(FP8X4), scales=y_scales[:, js], in_=y_bf[c][:, PACK * lo : PACK * hi]
             )
 
-        key_product(0)
         quantize_picks(last)
         w4_scales[1] = keep.tile([P, N], U8, name="w4_scales1", tag="xg_bf%d" % last, align_bytes=64)
         deal_scales(1, nc.gpsimd.tensor_copy)
-        for s in range(1, LEAD):
+        for s in range(LEAD):
             key_product(s)
         quantize_wvd()
         z_aside = keep.tile([P, 2, BANK], F32, name="z_aside", tag="wvd_bf", align_bytes=64)
@@ -296,9 +296,9 @@ def tile_list_dl_sigP_kernel(
             c, h = divmod(s, 2)
             value_step(s)
             if h == 1 and c < 2:
-                round_result_aside(c)
-            elif h == 1:
-                round_result(c, 0, HALF if c == last else CHUNK, nc.scalar.copy)
+                round_result_aside(c, CHUNK if c == 0 else HALF)
+            if h == 1 and c > 0:
+                round_result(c, HALF if c == 1 else 0, HALF if c == last else CHUNK, nc.scalar.copy)
         first_codes = keep.tile([P, 2 * CHUNK], U32, name="first_codes", tag="z%d" % (steps - 3), align_bytes=64)
         for c in range(2):
             y_codes[c] = first_codes[:, c * CHUNK : (c + 1) * CHUNK]

@@ -23,7 +23,7 @@ QUADRANTS = 4
 LIST_ROWS = 16
 BANK = 512
 CHUNK = 256
-NARROW = 128
+NARROW = 256
 HALF = CHUNK // 2
 DEPTH = 4
 LEAD = 4
@@ -167,7 +167,13 @@ def tile_list_dl_sigP_kernel(
             )
 
         def quantize_wvd():
-            nc.vector.quantize_mx(out=wvd_codes[:].bitcast(FP8X4), scales=wvd_scales[:], in_=wvd_bf[:])
+            for n0 in range(0, N, N // 2):
+                n1 = n0 + N // 2
+                nc.vector.quantize_mx(
+                    out=wvd_codes[:, n0:n1].bitcast(FP8X4),
+                    scales=wvd_scales[:, n0:n1],
+                    in_=wvd_bf[:, PACK * n0 : PACK * n1],
+                )
 
         deal_words()
         for i in range(2):
@@ -242,8 +248,8 @@ def tile_list_dl_sigP_kernel(
                     rhs, rhs_scale = xg_codes[c][:, js].bitcast(FP8X4), xg_scales[c][:, js]
                     nc.tensor.matmul_mx(
                         out=ve[:, u, js],
-                        lhsT=w4_words[:, 1, 2 * P * t : 2 * P * (t + 1)].bitcast(FP4X4),
-                        lhsT_scale=w4_scales[1][:, P * t : P * (t + 1)],
+                        lhsT=wvd_codes[:, P * t : P * (t + 1)].bitcast(FP8X4),
+                        lhsT_scale=wvd_scales[:, P * t : P * (t + 1)],
                         rhs=rhs,
                         rhs_scale=rhs_scale,
                         start=True,
@@ -251,8 +257,8 @@ def tile_list_dl_sigP_kernel(
                     )
                     nc.tensor.matmul_mx(
                         out=ve[:, u, js],
-                        lhsT=wvd_codes[:, P * t : P * (t + 1)].bitcast(FP8X4),
-                        lhsT_scale=wvd_scales[:, P * t : P * (t + 1)],
+                        lhsT=w4_words[:, 1, 2 * P * t : 2 * P * (t + 1)].bitcast(FP4X4),
+                        lhsT_scale=w4_scales[1][:, P * t : P * (t + 1)],
                         rhs=rhs,
                         rhs_scale=rhs_scale,
                         start=False,

@@ -27,6 +27,7 @@ NARROW = 256
 HALF = CHUNK // 2
 DEPTH = 4
 LEAD = 4
+ASIDE = 32
 BLOCKS = J // P
 REPEAT = 8
 
@@ -162,8 +163,12 @@ def tile_list_dl_sigP_kernel(
 
         def round_wvd():
             nc.scalar.copy(
-                out=wvd_bf[:].rearrange("p (h u m i) -> p h m i u", h=2, u=2, i=PACK),
-                in_=wvd_raw[:].rearrange("p i (m h u) -> p h m i u", h=2, u=2),
+                out=wvd_bf[:].rearrange("p (h u m i) -> p h m i u", h=2, u=2, i=PACK)[:, :, 0 : P - ASIDE],
+                in_=wvd_raw[:].rearrange("p i (m h u) -> p h m i u", h=2, u=2)[:, :, 0 : P - ASIDE],
+            )
+            nc.gpsimd.tensor_copy(
+                out=wvd_bf[:].rearrange("p (t m i) -> p m t i", t=PACK, i=PACK)[:, P - ASIDE :],
+                in_=wvd_raw[:].rearrange("p i (m t) -> p m t i", t=PACK)[:, P - ASIDE :],
             )
 
         def quantize_wvd():
@@ -198,12 +203,18 @@ def tile_list_dl_sigP_kernel(
         y_bf = {c: keep.tile([P, PACK * CHUNK], BF16, name="y_bf%d" % c, align_bytes=64) for c in range(1, chunks)}
         y_codes = {c: keep.tile([P, CHUNK], U32, name="y_codes%d" % c, align_bytes=64)[:] for c in range(2, chunks)}
         z = {s: keep.tile([P, BANK], F32, name="z%d" % s, align_bytes=64)[:] for s in range(steps - 2)}
-        gates = {s: z[s - 2] for s in range(2, steps)}
-        gates[0], gates[1] = wvd_raw[:, 2, :], wvd_raw[:, 3, :]
+        gates = {s: z[s - 2].rearrange("p (v j) -> p v j", j=P) for s in range(2, steps)}
+        gates[0], gates[1] = wvd_raw[:, :, 0:P], wvd_raw[:, :, P : 2 * P]
         ke = {}
 
         def by_slice(bank):
             return bank.rearrange("p (u j) -> p u j", u=2)
+
+        def by_quarter(bank):
+            return bank.rearrange("p (v j) -> p v j", j=P)
+
+        def quarters(rows):
+            return rows.rearrange("p u (v j) -> p (u v) j", j=P)
 
         def st_part(s):
             c, h = divmod(s, 2)
@@ -230,12 +241,12 @@ def tile_list_dl_sigP_kernel(
 
         def key_product_aside(s):
             key_matmuls(s)
-            keys = wvd_raw[:, s % 2, :]
-            nc.scalar.copy(out=keys, in_=ke[s][:])
-            nc.gpsimd.tensor_tensor(by_slice(z[s]), by_slice(keys), st_part(s), MULT)
+            keys = wvd_raw[:, :, (2 + s % 2) * P : (3 + s % 2) * P]
+            nc.scalar.copy(out=keys, in_=by_quarter(ke[s][:]))
+            nc.gpsimd.tensor_tensor(by_quarter(z[s]), keys, quarters(st_part(s)), MULT)
 
         def sigmoid(s):
-            nc.scalar.activation(out=gates[s], in_=z[s], func=SIGMOID)
+            nc.scalar.activation(out=gates[s], in_=by_quarter(z[s]), func=SIGMOID)
 
         def value_step(s):
             c, h = divmod(s, 2)
@@ -265,7 +276,7 @@ def tile_list_dl_sigP_kernel(
                         stop=True,
                     )
             result = y[c][:, 2 * h : 2 * h + 2, :]
-            nc.vector.tensor_tensor(result, ve, by_slice(gates[s]), MULT)
+            nc.vector.tensor_tensor(quarters(result), by_quarter(ve_bank[:]), gates[s], MULT)
             nc.sync.dma_start(out=out_rows[:, 2 * h : 2 * h + 2, c * CHUNK : (c + 1) * CHUNK], in_=result)
 
         def round_result(c, lo, hi, copy):
@@ -289,22 +300,24 @@ def tile_list_dl_sigP_kernel(
         for s in range(LEAD):
             key_product(s)
         quantize_wvd()
+        for s in range(2):
+            sigmoid(s)
         z_aside = keep.tile([P, 2, BANK], F32, name="z_aside", tag="wvd_bf", align_bytes=64)
         z[steps - 2], z[steps - 1] = z_aside[:, 0, :], z_aside[:, 1, :]
         for s in range(steps - 2, steps):
             key_product_aside(s)
         for s in range(LEAD, steps - 2):
             key_product(s)
-        for s in range(steps):
+        for s in range(2, steps):
             sigmoid(s)
         y_bf[0] = keep.tile([P, PACK * CHUNK], BF16, name="y_bf0", tag="state%d" % last, align_bytes=64)
         for s in range(steps):
             c, h = divmod(s, 2)
             value_step(s)
-            if h == 1 and c < 2:
-                round_result_aside(c, CHUNK if c == 0 else HALF)
+            if h == 1 and c == 0:
+                round_result_aside(c, CHUNK)
             if h == 1 and c > 0:
-                round_result(c, HALF if c == 1 else 0, HALF if c == last else CHUNK, nc.scalar.copy)
+                round_result(c, 0, HALF if c == last else CHUNK, nc.scalar.copy)
         first_codes = keep.tile([P, 2 * CHUNK], U32, name="first_codes", tag="z%d" % (steps - 3), align_bytes=64)
         for c in range(2):
             y_codes[c] = first_codes[:, c * CHUNK : (c + 1) * CHUNK]

@@ -26,8 +26,9 @@ CHUNK = 256
 NARROW = 256
 HALF = CHUNK // 2
 DEPTH = 4
-LEAD = 4
-ASIDE = 32
+LEAD = 3
+ASIDE_Y = 96
+ASIDE = 16
 BLOCKS = J // P
 REPEAT = 8
 
@@ -200,11 +201,10 @@ def tile_list_dl_sigP_kernel(
 
         y_scales = keep.tile([P, J], U8, name="y_scales", align_bytes=64)
         y = [keep.tile([P, PACK, CHUNK], F32, name="y%d" % c) for c in range(chunks)]
-        y_bf = {c: keep.tile([P, PACK * CHUNK], BF16, name="y_bf%d" % c, align_bytes=64) for c in range(1, chunks)}
-        y_codes = {c: keep.tile([P, CHUNK], U32, name="y_codes%d" % c, align_bytes=64)[:] for c in range(2, chunks)}
-        z = {s: keep.tile([P, BANK], F32, name="z%d" % s, align_bytes=64)[:] for s in range(steps - 2)}
-        gates = {s: z[s - 2].rearrange("p (v j) -> p v j", j=P) for s in range(2, steps)}
-        gates[0], gates[1] = wvd_raw[:, :, 0:P], wvd_raw[:, :, P : 2 * P]
+        y_bf = {c: keep.tile([P, PACK * CHUNK], BF16, name="y_bf%d" % c, align_bytes=64) for c in range(2, chunks)}
+        y_codes = {last: keep.tile([P, CHUNK], U32, name="y_codes%d" % last, align_bytes=64)[:]}
+        z = {s: keep.tile([P, BANK], F32, name="z%d" % s, align_bytes=64)[:] for s in range(LEAD)}
+        gates = {0: wvd_raw[:, :, 0:P], 1: wvd_raw[:, :, P : 2 * P]}
         ke = {}
 
         def by_slice(bank):
@@ -241,7 +241,7 @@ def tile_list_dl_sigP_kernel(
 
         def key_product_aside(s):
             key_matmuls(s)
-            keys = wvd_raw[:, :, (2 + s % 2) * P : (3 + s % 2) * P]
+            keys = keys_aside[s]
             nc.scalar.copy(out=keys, in_=by_quarter(ke[s][:]))
             nc.gpsimd.tensor_tensor(by_quarter(z[s]), keys, quarters(st_part(s)), MULT)
 
@@ -300,34 +300,49 @@ def tile_list_dl_sigP_kernel(
         for s in range(LEAD):
             key_product(s)
         quantize_wvd()
-        for s in range(2):
+        sigmoid(0)
+        z_next = keep.tile([P, 2, BANK], F32, name="z_next", tag="z0", align_bytes=64)
+        z[3], z[4] = z_next[:, 0, :], z_next[:, 1, :]
+        z[5] = keep.tile([P, BANK], F32, name="z5", tag="wvd_bf", align_bytes=64)[:]
+        z[6] = keep.tile([P, BANK], F32, name="z6", align_bytes=64)[:]
+        z[7] = z[1]
+        gates[2] = wvd_raw[:, :, 2 * P : 3 * P]
+        for s in range(3, steps - 1):
+            gates[s] = by_quarter(z[s - 2])
+        keys_aside = {5: wvd_raw[:, :, 3 * P : 4 * P]}
+        keys_aside[6] = by_quarter(keep.tile([P, BANK], F32, name="keys6", align_bytes=64)[:])
+        key_product(3)
+        key_product(4)
+        key_product_aside(5)
+        sigmoid(1)
+        key_product_aside(6)
+        for s in range(2, steps - 1):
             sigmoid(s)
-        z_aside = keep.tile([P, 2, BANK], F32, name="z_aside", tag="wvd_bf", align_bytes=64)
-        z[steps - 2], z[steps - 1] = z_aside[:, 0, :], z_aside[:, 1, :]
-        for s in range(steps - 2, steps):
-            key_product_aside(s)
-        for s in range(LEAD, steps - 2):
-            key_product(s)
-        for s in range(2, steps):
-            sigmoid(s)
-        y_bf[0] = keep.tile([P, PACK * CHUNK], BF16, name="y_bf0", tag="state%d" % last, align_bytes=64)
-        for s in range(steps):
-            c, h = divmod(s, 2)
+        y_bf[0] = keep.tile([P, PACK * CHUNK], BF16, name="y_bf0", tag="keys6", align_bytes=64)
+        y_bf[1] = keep.tile([P, PACK * CHUNK], BF16, name="y_bf1", tag="wvd_bf", align_bytes=64)
+        for s in range(5):
             value_step(s)
-            if h == 1 and c == 0:
-                round_result_aside(c, CHUNK)
-            if h == 1 and c > 0:
-                round_result(c, 0, HALF if c == last else CHUNK, nc.scalar.copy)
-        first_codes = keep.tile([P, 2 * CHUNK], U32, name="first_codes", tag="z%d" % (steps - 3), align_bytes=64)
-        for c in range(2):
+            if s == 1:
+                round_result_aside(0, CHUNK)
+            if s == 3:
+                round_result_aside(1, ASIDE_Y)
+        key_product(7)
+        gates[7] = by_quarter(keep.tile([P, BANK], F32, name="gate7", tag="z6", align_bytes=64)[:])
+        sigmoid(7)
+        round_result(1, ASIDE_Y, CHUNK, nc.scalar.copy)
+        value_step(5)
+        round_result(2, 0, CHUNK, nc.scalar.copy)
+        value_step(6)
+        value_step(7)
+        round_result(last, 0, HALF, nc.scalar.copy)
+        first_codes = keep.tile([P, last * CHUNK], U32, name="first_codes", tag="z0", align_bytes=64)
+        for c in range(last):
             y_codes[c] = first_codes[:, c * CHUNK : (c + 1) * CHUNK]
             quantize_result(c, 0, CHUNK)
-        nc.sync.dma_start(out=out_words[:, 0 : 2 * CHUNK], in_=first_codes[:].bitcast(I32))
+        nc.sync.dma_start(out=out_words[:, 0 : last * CHUNK], in_=first_codes[:].bitcast(I32))
         round_result(last, HALF, CHUNK, nc.vector.tensor_copy)
-        quantize_result(2, 0, CHUNK)
-        nc.sync.dma_start(out=out_words[:, 2 * CHUNK : 3 * CHUNK], in_=y_codes[2].bitcast(I32))
-        quantize_result(last, HALF, CHUNK)
         quantize_result(last, 0, HALF)
+        quantize_result(last, HALF, CHUNK)
 
         nc.scalar.dma_start(out=out_words[:, last * CHUNK : J], in_=y_codes[last].bitcast(I32))
         for q in range(QUADRANTS):

@@ -27,7 +27,7 @@ NARROW = 256
 HALF = CHUNK // 2
 DEPTH = 4
 LEAD = 3
-ASIDE_Y = 96
+ASIDE_Y = 144
 ASIDE = 16
 BLOCKS = J // P
 REPEAT = 8

@@ -23,12 +23,8 @@ QUADRANTS = 4
 LIST_ROWS = 16
 BANK = 512
 CHUNK = 256
-NARROW = 256
 HALF = CHUNK // 2
-DEPTH = 4
-LEAD = 3
-ASIDE_Y = 144
-ASIDE = 16
+ASIDE_Y = 128
 BLOCKS = J // P
 REPEAT = 8
 
@@ -56,33 +52,42 @@ def tile_list_dl_sigP_kernel(
 
     with ExitStack() as ctx:
         keep = ctx.enter_context(tc.tile_pool(name="keep", bufs=1))
-        ring = ctx.enter_context(tc.tile_pool(name="ring", bufs=DEPTH))
-        psum = ctx.enter_context(tc.psum_pool(name="psum", bufs=DEPTH))
+        ring = ctx.enter_context(tc.tile_pool(name="ring", bufs=chunks))
+        psum = ctx.enter_context(tc.psum_pool(name="psum", bufs=1))
+
+        def bank(number, name):
+            return psum.tile([P, BANK], F32, name=name, tag="bank%d" % number)
 
         offsets = keep.tile([P, J // LIST_ROWS], U16, name="offsets")
         raw_words = keep.tile([P, 2, 2 * N], U8, name="raw_words")
-        raw_scales = keep.tile([P, 2, N], U8, name="raw_scales")
+        raw_scales = [keep.tile([P, N], U8, name="raw_scales%d" % w, align_bytes=64) for w in range(2)]
         planes = [keep.tile([P, T], F32, name="plane%d" % i) for i in range(PACK)]
-        first_half = keep.tile([P, BANK], F32, name="first_half")
-        second_half = keep.tile([P, 3, CHUNK], F32, name="second_half")
-        weight = [first_half[:], second_half[:, 0:2, :].rearrange("p c j -> p (c j)")]
+        weight = [keep.tile([P, BANK], F32, name="weight%d" % h) for h in range(2)]
         weight_rows = keep.tile([P, P], F32, name="weight_rows")
         wvd_raw = keep.tile([P, PACK, N], F32, name="wvd_raw")
         identity = keep.tile([P, P], F32, name="identity")
-        state = [keep.tile([P, PACK, CHUNK], F32, name="state%d" % c, align_bytes=64) for c in range(chunks)]
+        state = [keep.tile([P, PACK, CHUNK], F32, name="state%d" % c) for c in range(last)]
+        last_state = [keep.tile([P, 2, CHUNK], F32, name="last_state%d" % h) for h in range(2)]
 
-        nc.gpsimd.memset(raw_scales[:].rearrange("p w n -> p (w n)").bitcast(I32), 0)
+        for w in range(2):
+            nc.gpsimd.memset(raw_scales[w][:].bitcast(I32), 0)
         make_identity(nc, identity[:])
 
         def load_scales(w, scales):
             for q in range(QUADRANTS):
                 nc.sync.dma_start(
-                    out=raw_scales[32 * q : 32 * q + 4, w, :].bitcast(I32),
+                    out=raw_scales[w][32 * q : 32 * q + 4, :].bitcast(I32),
                     in_=scales[0, 4 * q : 4 * q + 4, :].bitcast(I32),
                 )
 
         def load_plane(i):
             nc.sync.dma_start(out=planes[i][:], in_=x_rows[:, i, :])
+
+        def load_state(c):
+            nc.sync.dma_start(out=state[c][:], in_=st_rows[:, :, c * CHUNK : (c + 1) * CHUNK])
+
+        def load_last_state(h):
+            nc.sync.dma_start(out=last_state[h][:], in_=st_rows[:, 2 * h : 2 * h + 2, last * CHUNK : J])
 
         nc.sync.dma_start(out=weight_rows[:], in_=wgt.rearrange("(a b) (r j) -> a b r j", b=REPEAT, j=P)[:, 0, :, :])
         load_plane(0)
@@ -93,18 +98,20 @@ def tile_list_dl_sigP_kernel(
             nc.sync.dma_start(out=raw_words[:, w, :].bitcast(I32), in_=words[0].bitcast(I32))
         for i in range(2, PACK):
             load_plane(i)
+        nc.sync.dma_start(out=wvd_raw[:], in_=wvd.rearrange("(p i) n -> p i n", i=PACK))
+        load_state(0)
+        load_state(1)
         load_scales(1, wv4_scales)
-        for c in range(chunks):
-            nc.sync.dma_start(out=state[c][:], in_=st_rows[:, :, c * CHUNK : (c + 1) * CHUNK])
-            if c == 0:
-                nc.sync.dma_start(out=wvd_raw[:], in_=wvd.rearrange("(p i) n -> p i n", i=PACK))
+        load_last_state(0)
+        load_state(2)
+        load_last_state(1)
 
         warm = keep.tile([P, 1], F32, name="warm")
         nc.vector.memset(warm[:], 0.0)
         warm_out = keep.tile([P, 1], F32, name="warm_out")
         nc.scalar.activation(out=warm_out[:], in_=warm[:], func=SIGMOID)
 
-        turned = psum.tile([P, BANK], F32, name="turned", tag="ve")
+        turned = bank(4, "turned")
         nc.tensor.transpose(turned[:, 0:P], weight_rows[:], identity[:])
         by_block = turned[:, 0:P].rearrange("j (a r) -> j r a", r=BLOCKS)
         for c in range(chunks):
@@ -113,7 +120,7 @@ def tile_list_dl_sigP_kernel(
                 out=spread[:].rearrange("j r (a x) -> j r a x", x=REPEAT),
                 in_=by_block[:, 2 * c : 2 * c + 2, :].unsqueeze(3).to_broadcast([P, 2, P // REPEAT, REPEAT]),
             )
-            turned_back = psum.tile([P, BANK], F32, name="turned_back", tag="ke")
+            turned_back = bank(c, "turned_back")
             for r in range(2):
                 nc.tensor.transpose(turned_back[:, r * P : (r + 1) * P], spread[:, r, :], identity[:])
             nc.scalar.copy(out=weight[c // 2][:, c % 2 * CHUNK : (c % 2 + 1) * CHUNK], in_=turned_back[:, 0:CHUNK])
@@ -130,12 +137,14 @@ def tile_list_dl_sigP_kernel(
         def deal_scales(w, copy):
             copy(
                 out=w4_scales[w][:].rearrange("p (t m) -> p t m", t=PACK),
-                in_=raw_scales[:, w, :].rearrange("p (m t) -> p t m", t=PACK),
+                in_=raw_scales[w][:].rearrange("p (m t) -> p t m", t=PACK),
             )
 
         early = keep.tile([P, 2, J], F32, name="early")
-        pairs = [keep.tile([P, 2, CHUNK], F32, name="pair%d" % c)[:] for c in range(last)]
-        pairs.append(second_half[:, 0:3:2, :])
+        shared = keep.tile([P, 3, CHUNK], F32, name="shared")
+        pairs = {c: keep.tile([P, 2, CHUNK], F32, name="pair%d" % c)[:] for c in (0, 2)}
+        pairs[1] = shared[:, 0:2, :]
+        pairs[last] = shared[:, 0:3:2, :]
 
         def gather(out, i, j0, j1):
             nc.vector.tensor_tensor(
@@ -149,37 +158,20 @@ def tile_list_dl_sigP_kernel(
             gather(pairs[c][:, i - 2, :], i, c * CHUNK, (c + 1) * CHUNK)
 
         xg_codes = [keep.tile([P, CHUNK], U32, name="xg_codes%d" % c, align_bytes=64) for c in range(chunks)]
-        xg_scales = [keep.tile([P, CHUNK], U8, name="xg_scales%d" % c, align_bytes=64) for c in range(chunks)]
+        xg_scales = {c: keep.tile([P, CHUNK], U8, name="xg_scales%d" % c, align_bytes=64)[:] for c in range(last)}
         xg_bf = [keep.tile([P, PACK * CHUNK], BF16, name="xg_bf%d" % c, align_bytes=64) for c in range(chunks)]
 
         def round_picks(c, i, pair):
             nc.scalar.copy(out=woven(xg_bf[c][:])[:, :, i : i + 2, :], in_=weave(pair))
 
-        def quantize_picks(c):
-            nc.vector.quantize_mx(out=xg_codes[c][:].bitcast(FP8X4), scales=xg_scales[c][:], in_=xg_bf[c][:])
-
-        wvd_bf = keep.tile([P, PACK * N], BF16, name="wvd_bf", align_bytes=64)
-        wvd_codes = keep.tile([P, N], U32, name="wvd_codes", align_bytes=64)
-        wvd_scales = keep.tile([P, N], U8, name="wvd_scales", align_bytes=64)
-
-        def round_wvd():
-            nc.scalar.copy(
-                out=wvd_bf[:].rearrange("p (h u m i) -> p h m i u", h=2, u=2, i=PACK)[:, :, 0 : P - ASIDE],
-                in_=wvd_raw[:].rearrange("p i (m h u) -> p h m i u", h=2, u=2)[:, :, 0 : P - ASIDE],
-            )
+        def round_picks_aside(c, i, pair):
             nc.gpsimd.tensor_copy(
-                out=wvd_bf[:].rearrange("p (t m i) -> p m t i", t=PACK, i=PACK)[:, P - ASIDE :],
-                in_=wvd_raw[:].rearrange("p i (m t) -> p m t i", t=PACK)[:, P - ASIDE :],
+                out=xg_bf[c][:].rearrange("p (j t) -> p j t", t=PACK)[:, :, i : i + 2],
+                in_=pair.rearrange("p t j -> p j t"),
             )
 
-        def quantize_wvd():
-            for n0 in range(0, N, N // 2):
-                n1 = n0 + N // 2
-                nc.vector.quantize_mx(
-                    out=wvd_codes[:, n0:n1].bitcast(FP8X4),
-                    scales=wvd_scales[:, n0:n1],
-                    in_=wvd_bf[:, PACK * n0 : PACK * n1],
-                )
+        def quantize_picks(c):
+            nc.vector.quantize_mx(out=xg_codes[c][:].bitcast(FP8X4), scales=xg_scales[c], in_=xg_bf[c][:])
 
         deal_words()
         for i in range(2):
@@ -191,96 +183,109 @@ def tile_list_dl_sigP_kernel(
             gather_late(2, c)
         for c in range(chunks):
             gather_late(3, c)
-            if c == last:
-                gather_late(2, c)
+        for c in range(last):
             round_picks(c, 2, pairs[c])
         deal_scales(0, nc.vector.tensor_copy)
-        for c in range(last):
-            quantize_picks(c)
-        round_wvd()
+        quantize_picks(0)
+        quantize_picks(1)
+        gather_late(2, last)
+        quantize_picks(2)
+        round_picks_aside(last, 2, pairs[last])
+        w4_scales[1] = keep.tile([P, N], U8, name="w4_scales1", tag="xg_bf2", align_bytes=64)
+        deal_scales(1, nc.gpsimd.tensor_copy)
+
+        wvd_bf = keep.tile([P, PACK * N], BF16, name="wvd_bf", tag="xg_bf0", align_bytes=64)
+        wvd_codes = keep.tile([P, N], U32, name="wvd_codes", align_bytes=64)
+        nc.scalar.copy(
+            out=wvd_bf[:].rearrange("p (h u m i) -> p h m i u", h=2, u=2, i=PACK),
+            in_=wvd_raw[:].rearrange("p i (m h u) -> p h m i u", h=2, u=2),
+        )
+        late_scales = keep.tile([P, CHUNK + N], U8, name="late_scales", tag="raw_scales1", align_bytes=64)
+        xg_scales[last] = late_scales[:, 0:CHUNK]
+        wvd_scales = late_scales[:, CHUNK : CHUNK + N]
+
+        def quantize_wvd():
+            for n0 in range(0, N, N // 2):
+                n1 = n0 + N // 2
+                nc.vector.quantize_mx(
+                    out=wvd_codes[:, n0:n1].bitcast(FP8X4),
+                    scales=wvd_scales[:, n0:n1],
+                    in_=wvd_bf[:, PACK * n0 : PACK * n1],
+                )
 
         y_scales = keep.tile([P, J], U8, name="y_scales", align_bytes=64)
         y = [keep.tile([P, PACK, CHUNK], F32, name="y%d" % c) for c in range(chunks)]
-        y_bf = {c: keep.tile([P, PACK * CHUNK], BF16, name="y_bf%d" % c, align_bytes=64) for c in range(2, chunks)}
-        y_codes = {last: keep.tile([P, CHUNK], U32, name="y_codes%d" % last, align_bytes=64)[:]}
-        z = {s: keep.tile([P, BANK], F32, name="z%d" % s, align_bytes=64)[:] for s in range(LEAD)}
-        gates = {0: wvd_raw[:, :, 0:P], 1: wvd_raw[:, :, P : 2 * P]}
-        ke = {}
+        y_bf = {c: keep.tile([P, PACK * CHUNK], BF16, name="y_bf%d" % c, align_bytes=64)[:] for c in range(2, chunks)}
+        z = {s: keep.tile([P, BANK], F32, name="z%d" % s, align_bytes=64)[:] for s in range(steps) if s != 4}
+        gates = {s: keep.tile([P, BANK], F32, name="gate%d" % s, align_bytes=64)[:] for s in range(steps - 1)}
+        keys = {s: keep.tile([P, BANK], F32, name="keys%d" % s, align_bytes=64)[:] for s in (4, 5)}
+        key_bank = (0, 1, 2, 3, 0, 1, 2, 4)
+        value_bank = (4, 5, 6, 7, 3, 5, 6, 7)
 
-        def by_slice(bank):
-            return bank.rearrange("p (u j) -> p u j", u=2)
-
-        def by_quarter(bank):
-            return bank.rearrange("p (v j) -> p v j", j=P)
-
-        def quarters(rows):
-            return rows.rearrange("p u (v j) -> p (u v) j", j=P)
+        def by_slice(flat):
+            return flat.rearrange("p (u j) -> p u j", u=2)
 
         def st_part(s):
             c, h = divmod(s, 2)
-            return state[c][:, 2 * h : 2 * h + 2, :]
+            rows = last_state[h][:] if c == last else state[c][:, 2 * h : 2 * h + 2, :]
+            return rows.rearrange("p u j -> p (u j)")
 
         def key_matmuls(s):
             c, h = divmod(s, 2)
-            ke[s] = psum.tile([P, BANK], F32, name="ke")
+            ke = bank(key_bank[s], "ke")
             for u in range(2):
                 t = 2 * h + u
                 nc.tensor.matmul_mx(
-                    out=by_slice(ke[s][:])[:, u, :],
+                    out=by_slice(ke[:])[:, u, :],
                     lhsT=w4_words[:, 0, 2 * P * t : 2 * P * (t + 1)].bitcast(FP4X4),
                     lhsT_scale=w4_scales[0][:, P * t : P * (t + 1)],
                     rhs=xg_codes[c][:].bitcast(FP8X4),
-                    rhs_scale=xg_scales[c][:],
+                    rhs_scale=xg_scales[c],
                     start=True,
                     stop=True,
                 )
+            return ke[:]
 
         def key_product(s):
-            key_matmuls(s)
-            nc.vector.tensor_tensor(by_slice(z[s]), by_slice(ke[s][:]), st_part(s), MULT)
+            nc.vector.tensor_tensor(z[s], key_matmuls(s), st_part(s), MULT)
 
         def key_product_aside(s):
-            key_matmuls(s)
-            keys = keys_aside[s]
-            nc.scalar.copy(out=keys, in_=by_quarter(ke[s][:]))
-            nc.gpsimd.tensor_tensor(by_quarter(z[s]), keys, quarters(st_part(s)), MULT)
+            nc.scalar.copy(out=keys[s], in_=key_matmuls(s))
+            nc.gpsimd.tensor_tensor(z[s], keys[s], st_part(s), MULT)
 
         def sigmoid(s):
-            nc.scalar.activation(out=gates[s], in_=by_quarter(z[s]), func=SIGMOID)
+            nc.scalar.activation(out=gates[s], in_=z[s], func=SIGMOID)
 
         def value_step(s):
             c, h = divmod(s, 2)
-            ve_bank = psum.tile([P, BANK], F32, name="ve_bank", tag="ve")
-            ve = by_slice(ve_bank[:])
+            ve = bank(value_bank[s], "ve")
+            rhs, rhs_scale = xg_codes[c][:].bitcast(FP8X4), xg_scales[c]
             for u in range(2):
                 t = 2 * h + u
-                for j0 in range(0, CHUNK, NARROW):
-                    js = slice(j0, j0 + NARROW)
-                    rhs, rhs_scale = xg_codes[c][:, js].bitcast(FP8X4), xg_scales[c][:, js]
-                    nc.tensor.matmul_mx(
-                        out=ve[:, u, js],
-                        lhsT=wvd_codes[:, P * t : P * (t + 1)].bitcast(FP8X4),
-                        lhsT_scale=wvd_scales[:, P * t : P * (t + 1)],
-                        rhs=rhs,
-                        rhs_scale=rhs_scale,
-                        start=True,
-                        stop=False,
-                    )
-                    nc.tensor.matmul_mx(
-                        out=ve[:, u, js],
-                        lhsT=w4_words[:, 1, 2 * P * t : 2 * P * (t + 1)].bitcast(FP4X4),
-                        lhsT_scale=w4_scales[1][:, P * t : P * (t + 1)],
-                        rhs=rhs,
-                        rhs_scale=rhs_scale,
-                        start=False,
-                        stop=True,
-                    )
+                nc.tensor.matmul_mx(
+                    out=by_slice(ve[:])[:, u, :],
+                    lhsT=wvd_codes[:, P * t : P * (t + 1)].bitcast(FP8X4),
+                    lhsT_scale=wvd_scales[:, P * t : P * (t + 1)],
+                    rhs=rhs,
+                    rhs_scale=rhs_scale,
+                    start=True,
+                    stop=False,
+                )
+                nc.tensor.matmul_mx(
+                    out=by_slice(ve[:])[:, u, :],
+                    lhsT=w4_words[:, 1, 2 * P * t : 2 * P * (t + 1)].bitcast(FP4X4),
+                    lhsT_scale=w4_scales[1][:, P * t : P * (t + 1)],
+                    rhs=rhs,
+                    rhs_scale=rhs_scale,
+                    start=False,
+                    stop=True,
+                )
             result = y[c][:, 2 * h : 2 * h + 2, :]
-            nc.vector.tensor_tensor(quarters(result), by_quarter(ve_bank[:]), gates[s], MULT)
+            nc.vector.tensor_tensor(result.rearrange("p u j -> p (u j)"), ve[:], gates[s], MULT)
             nc.sync.dma_start(out=out_rows[:, 2 * h : 2 * h + 2, c * CHUNK : (c + 1) * CHUNK], in_=result)
 
-        def round_result(c, lo, hi, copy):
-            copy(out=woven(y_bf[c][:, PACK * lo : PACK * hi]), in_=weave(y[c][:, :, lo:hi]))
+        def round_result(c, lo, hi):
+            nc.scalar.copy(out=woven(y_bf[c][:, PACK * lo : PACK * hi]), in_=weave(y[c][:, :, lo:hi]))
 
         def round_result_aside(c, hi):
             nc.gpsimd.tensor_copy(
@@ -288,63 +293,54 @@ def tile_list_dl_sigP_kernel(
                 in_=y[c][:, :, 0:hi].rearrange("p t j -> p j t"),
             )
 
-        def quantize_result(c, lo, hi):
-            js = slice(c * CHUNK + lo, c * CHUNK + hi)
-            nc.vector.quantize_mx(
-                out=y_codes[c][:, lo:hi].bitcast(FP8X4), scales=y_scales[:, js], in_=y_bf[c][:, PACK * lo : PACK * hi]
-            )
-
-        quantize_picks(last)
-        w4_scales[1] = keep.tile([P, N], U8, name="w4_scales1", tag="xg_bf%d" % last, align_bytes=64)
-        deal_scales(1, nc.gpsimd.tensor_copy)
-        for s in range(LEAD):
+        for s in range(4):
             key_product(s)
+        quantize_picks(last)
         quantize_wvd()
+        z[4] = keep.tile([P, BANK], F32, name="z4", tag="xg_bf0", align_bytes=64)[:]
         sigmoid(0)
-        z_next = keep.tile([P, 2, BANK], F32, name="z_next", tag="z0", align_bytes=64)
-        z[3], z[4] = z_next[:, 0, :], z_next[:, 1, :]
-        z[5] = keep.tile([P, BANK], F32, name="z5", tag="wvd_bf", align_bytes=64)[:]
-        z[6] = keep.tile([P, BANK], F32, name="z6", align_bytes=64)[:]
-        z[7] = z[1]
-        gates[2] = wvd_raw[:, :, 2 * P : 3 * P]
-        for s in range(3, steps - 1):
-            gates[s] = by_quarter(z[s - 2])
-        keys_aside = {5: wvd_raw[:, :, 3 * P : 4 * P]}
-        keys_aside[6] = by_quarter(keep.tile([P, BANK], F32, name="keys6", align_bytes=64)[:])
-        key_product(3)
-        key_product(4)
-        key_product_aside(5)
         sigmoid(1)
-        key_product_aside(6)
-        for s in range(2, steps - 1):
+        key_product_aside(4)
+        sigmoid(2)
+        key_product_aside(5)
+        key_product(6)
+        for s in (3, 4, 6, 5):
             sigmoid(s)
-        y_bf[0] = keep.tile([P, PACK * CHUNK], BF16, name="y_bf0", tag="keys6", align_bytes=64)
-        y_bf[1] = keep.tile([P, PACK * CHUNK], BF16, name="y_bf1", tag="wvd_bf", align_bytes=64)
+        first_bf = keep.tile([P, 2 * PACK * CHUNK], BF16, name="first_bf", tag="keys5", align_bytes=64)
+        for c in range(2):
+            y_bf[c] = first_bf[:, c * PACK * CHUNK : (c + 1) * PACK * CHUNK]
         for s in range(5):
             value_step(s)
             if s == 1:
                 round_result_aside(0, CHUNK)
             if s == 3:
-                round_result_aside(1, ASIDE_Y)
+                round_result(1, 0, CHUNK)
         key_product(7)
-        gates[7] = by_quarter(keep.tile([P, BANK], F32, name="gate7", tag="z6", align_bytes=64)[:])
+        gates[7] = keep.tile([P, BANK], F32, name="gate7", tag="z5", align_bytes=64)[:]
         sigmoid(7)
-        round_result(1, ASIDE_Y, CHUNK, nc.scalar.copy)
         value_step(5)
-        round_result(2, 0, CHUNK, nc.scalar.copy)
+        round_result_aside(2, ASIDE_Y)
+        round_result(2, ASIDE_Y, CHUNK)
         value_step(6)
         value_step(7)
-        round_result(last, 0, HALF, nc.scalar.copy)
-        first_codes = keep.tile([P, last * CHUNK], U32, name="first_codes", tag="z0", align_bytes=64)
+        round_result(last, 0, HALF)
+        round_result(last, HALF, CHUNK)
+
+        y_codes = keep.tile([P, J], U32, name="y_codes", tag="gate6", align_bytes=64)
+
+        def quantize_result(c, lo, hi):
+            js = slice(c * CHUNK + lo, c * CHUNK + hi)
+            nc.vector.quantize_mx(
+                out=y_codes[:, js].bitcast(FP8X4), scales=y_scales[:, js], in_=y_bf[c][:, PACK * lo : PACK * hi]
+            )
+
         for c in range(last):
-            y_codes[c] = first_codes[:, c * CHUNK : (c + 1) * CHUNK]
             quantize_result(c, 0, CHUNK)
-        nc.sync.dma_start(out=out_words[:, 0 : last * CHUNK], in_=first_codes[:].bitcast(I32))
-        round_result(last, HALF, CHUNK, nc.vector.tensor_copy)
+        nc.sync.dma_start(out=out_words[:, 0 : last * CHUNK], in_=y_codes[:, 0 : last * CHUNK].bitcast(I32))
         quantize_result(last, 0, HALF)
         quantize_result(last, HALF, CHUNK)
 
-        nc.scalar.dma_start(out=out_words[:, last * CHUNK : J], in_=y_codes[last].bitcast(I32))
+        nc.scalar.dma_start(out=out_words[:, last * CHUNK : J], in_=y_codes[:, last * CHUNK : J].bitcast(I32))
         for q in range(QUADRANTS):
             queue = nc.sync if q % 2 == 0 else nc.scalar
             queue.dma_start(out=out_scales[4 * q : 4 * q + 4, :], in_=y_scales[32 * q : 32 * q + 4, :].bitcast(I32))

@@ -25,6 +25,7 @@ BANK = 512
 CHUNK = 256
 HALF = CHUNK // 2
 ASIDE_Y = 128
+OWN_Y = 64
 BLOCKS = J // P
 REPEAT = 8
 
@@ -66,8 +67,7 @@ def tile_list_dl_sigP_kernel(
         weight_rows = keep.tile([P, P], F32, name="weight_rows")
         wvd_raw = keep.tile([P, PACK, N], F32, name="wvd_raw")
         identity = keep.tile([P, P], F32, name="identity")
-        state = [keep.tile([P, PACK, CHUNK], F32, name="state%d" % c) for c in range(last)]
-        last_state = [keep.tile([P, 2, CHUNK], F32, name="last_state%d" % h) for h in range(2)]
+        state = [keep.tile([P, BANK], F32, name="state%d" % s, align_bytes=64)[:] for s in range(steps)]
 
         for w in range(2):
             nc.gpsimd.memset(raw_scales[w][:].bitcast(I32), 0)
@@ -83,11 +83,12 @@ def tile_list_dl_sigP_kernel(
         def load_plane(i):
             nc.sync.dma_start(out=planes[i][:], in_=x_rows[:, i, :])
 
-        def load_state(c):
-            nc.sync.dma_start(out=state[c][:], in_=st_rows[:, :, c * CHUNK : (c + 1) * CHUNK])
-
-        def load_last_state(h):
-            nc.sync.dma_start(out=last_state[h][:], in_=st_rows[:, 2 * h : 2 * h + 2, last * CHUNK : J])
+        def load_state(s):
+            c, h = divmod(s, 2)
+            nc.sync.dma_start(
+                out=state[s].rearrange("p (t j) -> p t j", t=2),
+                in_=st_rows[:, 2 * h : 2 * h + 2, c * CHUNK : (c + 1) * CHUNK],
+            )
 
         nc.sync.dma_start(out=weight_rows[:], in_=wgt.rearrange("(a b) (r j) -> a b r j", b=REPEAT, j=P)[:, 0, :, :])
         load_plane(0)
@@ -98,13 +99,11 @@ def tile_list_dl_sigP_kernel(
             nc.sync.dma_start(out=raw_words[:, w, :].bitcast(I32), in_=words[0].bitcast(I32))
         for i in range(2, PACK):
             load_plane(i)
-        nc.sync.dma_start(out=wvd_raw[:], in_=wvd.rearrange("(p i) n -> p i n", i=PACK))
-        load_state(0)
-        load_state(1)
         load_scales(1, wv4_scales)
-        load_last_state(0)
-        load_state(2)
-        load_last_state(1)
+        load_state(0)
+        nc.sync.dma_start(out=wvd_raw[:], in_=wvd.rearrange("(p i) n -> p i n", i=PACK))
+        for s in (1, 2, 3, 4, 6, 5, 7):
+            load_state(s)
 
         warm = keep.tile([P, 1], F32, name="warm")
         nc.vector.memset(warm[:], 0.0)
@@ -157,8 +156,8 @@ def tile_list_dl_sigP_kernel(
         def gather_late(i, c):
             gather(pairs[c][:, i - 2, :], i, c * CHUNK, (c + 1) * CHUNK)
 
-        xg_codes = [keep.tile([P, CHUNK], U32, name="xg_codes%d" % c, align_bytes=64) for c in range(chunks)]
-        xg_scales = {c: keep.tile([P, CHUNK], U8, name="xg_scales%d" % c, align_bytes=64)[:] for c in range(last)}
+        xg_codes = [keep.tile([P, CHUNK], U32, name="xg_codes%d" % c, align_bytes=64)[:] for c in range(last)]
+        xg_scales = [keep.tile([P, CHUNK], U8, name="xg_scales%d" % c, align_bytes=64)[:] for c in range(chunks)]
         xg_bf = [keep.tile([P, PACK * CHUNK], BF16, name="xg_bf%d" % c, align_bytes=64) for c in range(chunks)]
 
         def round_picks(c, i, pair):
@@ -171,7 +170,7 @@ def tile_list_dl_sigP_kernel(
             )
 
         def quantize_picks(c):
-            nc.vector.quantize_mx(out=xg_codes[c][:].bitcast(FP8X4), scales=xg_scales[c], in_=xg_bf[c][:])
+            nc.vector.quantize_mx(out=xg_codes[c].bitcast(FP8X4), scales=xg_scales[c], in_=xg_bf[c][:])
 
         deal_words()
         for i in range(2):
@@ -195,14 +194,11 @@ def tile_list_dl_sigP_kernel(
         deal_scales(1, nc.gpsimd.tensor_copy)
 
         wvd_bf = keep.tile([P, PACK * N], BF16, name="wvd_bf", tag="xg_bf0", align_bytes=64)
-        wvd_codes = keep.tile([P, N], U32, name="wvd_codes", align_bytes=64)
+        wvd_scales = keep.tile([P, N], U8, name="wvd_scales", align_bytes=64)
         nc.scalar.copy(
             out=wvd_bf[:].rearrange("p (h u m i) -> p h m i u", h=2, u=2, i=PACK),
             in_=wvd_raw[:].rearrange("p i (m h u) -> p h m i u", h=2, u=2),
         )
-        late_scales = keep.tile([P, CHUNK + N], U8, name="late_scales", tag="raw_scales1", align_bytes=64)
-        xg_scales[last] = late_scales[:, 0:CHUNK]
-        wvd_scales = late_scales[:, CHUNK : CHUNK + N]
 
         def quantize_wvd():
             for n0 in range(0, N, N // 2):
@@ -217,18 +213,13 @@ def tile_list_dl_sigP_kernel(
         y = [keep.tile([P, PACK, CHUNK], F32, name="y%d" % c) for c in range(chunks)]
         y_bf = {c: keep.tile([P, PACK * CHUNK], BF16, name="y_bf%d" % c, align_bytes=64)[:] for c in range(2, chunks)}
         z = {s: keep.tile([P, BANK], F32, name="z%d" % s, align_bytes=64)[:] for s in range(steps) if s != 4}
-        gates = {s: keep.tile([P, BANK], F32, name="gate%d" % s, align_bytes=64)[:] for s in range(steps - 1)}
+        gates = {s: keep.tile([P, BANK], F32, name="gate%d" % s, align_bytes=64)[:] for s in range(1, steps - 1)}
         keys = {s: keep.tile([P, BANK], F32, name="keys%d" % s, align_bytes=64)[:] for s in (4, 5)}
-        key_bank = (0, 1, 2, 3, 0, 1, 2, 4)
+        key_bank = (0, 1, 2, 3, 1, 2, 0, 4)
         value_bank = (4, 5, 6, 7, 3, 5, 6, 7)
 
         def by_slice(flat):
             return flat.rearrange("p (u j) -> p u j", u=2)
-
-        def st_part(s):
-            c, h = divmod(s, 2)
-            rows = last_state[h][:] if c == last else state[c][:, 2 * h : 2 * h + 2, :]
-            return rows.rearrange("p u j -> p (u j)")
 
         def key_matmuls(s):
             c, h = divmod(s, 2)
@@ -239,7 +230,7 @@ def tile_list_dl_sigP_kernel(
                     out=by_slice(ke[:])[:, u, :],
                     lhsT=w4_words[:, 0, 2 * P * t : 2 * P * (t + 1)].bitcast(FP4X4),
                     lhsT_scale=w4_scales[0][:, P * t : P * (t + 1)],
-                    rhs=xg_codes[c][:].bitcast(FP8X4),
+                    rhs=xg_codes[c].bitcast(FP8X4),
                     rhs_scale=xg_scales[c],
                     start=True,
                     stop=True,
@@ -247,11 +238,11 @@ def tile_list_dl_sigP_kernel(
             return ke[:]
 
         def key_product(s):
-            nc.vector.tensor_tensor(z[s], key_matmuls(s), st_part(s), MULT)
+            nc.vector.tensor_tensor(z[s], key_matmuls(s), state[s], MULT)
 
         def key_product_aside(s):
             nc.scalar.copy(out=keys[s], in_=key_matmuls(s))
-            nc.gpsimd.tensor_tensor(z[s], keys[s], st_part(s), MULT)
+            nc.gpsimd.tensor_tensor(z[s], keys[s], state[s], MULT)
 
         def sigmoid(s):
             nc.scalar.activation(out=gates[s], in_=z[s], func=SIGMOID)
@@ -259,7 +250,7 @@ def tile_list_dl_sigP_kernel(
         def value_step(s):
             c, h = divmod(s, 2)
             ve = bank(value_bank[s], "ve")
-            rhs, rhs_scale = xg_codes[c][:].bitcast(FP8X4), xg_scales[c]
+            rhs, rhs_scale = xg_codes[c].bitcast(FP8X4), xg_scales[c]
             for u in range(2):
                 t = 2 * h + u
                 nc.tensor.matmul_mx(
@@ -284,8 +275,8 @@ def tile_list_dl_sigP_kernel(
             nc.vector.tensor_tensor(result.rearrange("p u j -> p (u j)"), ve[:], gates[s], MULT)
             nc.sync.dma_start(out=out_rows[:, 2 * h : 2 * h + 2, c * CHUNK : (c + 1) * CHUNK], in_=result)
 
-        def round_result(c, lo, hi):
-            nc.scalar.copy(out=woven(y_bf[c][:, PACK * lo : PACK * hi]), in_=weave(y[c][:, :, lo:hi]))
+        def round_result(c, lo, hi, copy=nc.scalar.copy):
+            copy(out=woven(y_bf[c][:, PACK * lo : PACK * hi]), in_=weave(y[c][:, :, lo:hi]))
 
         def round_result_aside(c, hi):
             nc.gpsimd.tensor_copy(
@@ -295,9 +286,12 @@ def tile_list_dl_sigP_kernel(
 
         for s in range(4):
             key_product(s)
+        xg_codes.append(keep.tile([P, CHUNK], U32, name="last_codes", tag="state2", align_bytes=64)[:])
+        wvd_codes = keep.tile([P, N], U32, name="wvd_codes", tag="state3", align_bytes=64)
         quantize_picks(last)
         quantize_wvd()
         z[4] = keep.tile([P, BANK], F32, name="z4", tag="xg_bf0", align_bytes=64)[:]
+        gates[0] = keep.tile([P, BANK], F32, name="gate0", tag="state1", align_bytes=64)[:]
         sigmoid(0)
         sigmoid(1)
         key_product_aside(4)
@@ -324,9 +318,9 @@ def tile_list_dl_sigP_kernel(
         value_step(6)
         value_step(7)
         round_result(last, 0, HALF)
-        round_result(last, HALF, CHUNK)
+        round_result(last, HALF, CHUNK - OWN_Y)
 
-        y_codes = keep.tile([P, J], U32, name="y_codes", tag="gate6", align_bytes=64)
+        y_codes = keep.tile([P, J], U32, name="y_codes", tag="z7", align_bytes=64)
 
         def quantize_result(c, lo, hi):
             js = slice(c * CHUNK + lo, c * CHUNK + hi)
@@ -337,6 +331,7 @@ def tile_list_dl_sigP_kernel(
         for c in range(last):
             quantize_result(c, 0, CHUNK)
         nc.sync.dma_start(out=out_words[:, 0 : last * CHUNK], in_=y_codes[:, 0 : last * CHUNK].bitcast(I32))
+        round_result(last, CHUNK - OWN_Y, CHUNK, nc.vector.tensor_copy)
         quantize_result(last, 0, HALF)
         quantize_result(last, HALF, CHUNK)
 

@@ -24,7 +24,7 @@ LIST_ROWS = 16
 BANK = 512
 CHUNK = 256
 HALF = CHUNK // 2
-ASIDE_Y = 128
+ASIDE_Y = 160
 OWN_Y = 64
 BLOCKS = J // P
 REPEAT = 8
@@ -193,21 +193,20 @@ def tile_list_dl_sigP_kernel(
         w4_scales[1] = keep.tile([P, N], U8, name="w4_scales1", tag="xg_bf2", align_bytes=64)
         deal_scales(1, nc.gpsimd.tensor_copy)
 
-        wvd_bf = keep.tile([P, PACK * N], BF16, name="wvd_bf", tag="xg_bf0", align_bytes=64)
+        wvd_bf = [
+            keep.tile([P, 2 * N], BF16, name="wvd_bf%d" % h, tag="xg_bf%d" % h, align_bytes=64) for h in range(2)
+        ]
         wvd_scales = keep.tile([P, N], U8, name="wvd_scales", align_bytes=64)
-        nc.scalar.copy(
-            out=wvd_bf[:].rearrange("p (h u m i) -> p h m i u", h=2, u=2, i=PACK),
-            in_=wvd_raw[:].rearrange("p i (m h u) -> p h m i u", h=2, u=2),
-        )
+        for h in range(2):
+            nc.scalar.copy(
+                out=wvd_bf[h][:].rearrange("p (u m i) -> p m i u", u=2, i=PACK),
+                in_=wvd_raw[:].rearrange("p i (m h u) -> p h m i u", h=2, u=2)[:, h],
+            )
 
         def quantize_wvd():
-            for n0 in range(0, N, N // 2):
-                n1 = n0 + N // 2
-                nc.vector.quantize_mx(
-                    out=wvd_codes[:, n0:n1].bitcast(FP8X4),
-                    scales=wvd_scales[:, n0:n1],
-                    in_=wvd_bf[:, PACK * n0 : PACK * n1],
-                )
+            for h in range(2):
+                ns = slice(h * N // 2, (h + 1) * N // 2)
+                nc.vector.quantize_mx(out=wvd_codes[:, ns].bitcast(FP8X4), scales=wvd_scales[:, ns], in_=wvd_bf[h][:])
 
         y_scales = keep.tile([P, J], U8, name="y_scales", align_bytes=64)
         y = [keep.tile([P, PACK, CHUNK], F32, name="y%d" % c) for c in range(chunks)]
@@ -308,13 +307,13 @@ def tile_list_dl_sigP_kernel(
             if s == 1:
                 round_result_aside(0, CHUNK)
             if s == 3:
-                round_result(1, 0, CHUNK)
+                round_result_aside(1, ASIDE_Y)
+                round_result(1, ASIDE_Y, CHUNK)
         key_product(7)
         gates[7] = keep.tile([P, BANK], F32, name="gate7", tag="z5", align_bytes=64)[:]
         sigmoid(7)
         value_step(5)
-        round_result_aside(2, ASIDE_Y)
-        round_result(2, ASIDE_Y, CHUNK)
+        round_result(2, 0, CHUNK)
         value_step(6)
         value_step(7)
         round_result(last, 0, HALF)

@@ -24,7 +24,7 @@ LIST_ROWS = 16
 BANK = 512
 CHUNK = 256
 HALF = CHUNK // 2
-ASIDE_Y = 160
+ASIDE_Y = 112
 OWN_Y = 64
 BLOCKS = J // P
 REPEAT = 8
@@ -213,9 +213,10 @@ def tile_list_dl_sigP_kernel(
         y_bf = {c: keep.tile([P, PACK * CHUNK], BF16, name="y_bf%d" % c, align_bytes=64)[:] for c in range(2, chunks)}
         z = {s: keep.tile([P, BANK], F32, name="z%d" % s, align_bytes=64)[:] for s in range(steps) if s != 4}
         gates = {s: keep.tile([P, BANK], F32, name="gate%d" % s, align_bytes=64)[:] for s in range(1, steps - 1)}
-        keys = {s: keep.tile([P, BANK], F32, name="keys%d" % s, align_bytes=64)[:] for s in (4, 5)}
-        key_bank = (0, 1, 2, 3, 1, 2, 0, 4)
-        value_bank = (4, 5, 6, 7, 3, 5, 6, 7)
+        keys = {}
+        key_bank = (0, 1, 2, 3, 4, 5, 0, 1)
+        value_bank = (1, 2, 3, 6, 7, 4, 5, 0)
+        ve = {}
 
         def by_slice(flat):
             return flat.rearrange("p (u j) -> p u j", u=2)
@@ -246,32 +247,43 @@ def tile_list_dl_sigP_kernel(
         def sigmoid(s):
             nc.scalar.activation(out=gates[s], in_=z[s], func=SIGMOID)
 
+        def value_pass(s, u, words, scales, start, stop):
+            c, h = divmod(s, 2)
+            nc.tensor.matmul_mx(
+                out=by_slice(ve[s][:])[:, u, :],
+                lhsT=words,
+                lhsT_scale=scales[:, P * (2 * h + u) : P * (2 * h + u + 1)],
+                rhs=xg_codes[c].bitcast(FP8X4),
+                rhs_scale=xg_scales[c],
+                start=start,
+                stop=stop,
+            )
+
+        def base_pass(s, u, start, stop):
+            t = 2 * (s % 2) + u
+            value_pass(s, u, w4_words[:, 1, 2 * P * t : 2 * P * (t + 1)].bitcast(FP4X4), w4_scales[1], start, stop)
+
+        def change_pass(s, u, start, stop):
+            t = 2 * (s % 2) + u
+            value_pass(s, u, wvd_codes[:, P * t : P * (t + 1)].bitcast(FP8X4), wvd_scales, start, stop)
+
+        def base_ahead(s):
+            ve[s] = bank(value_bank[s], "ve")
+            for u in range(2):
+                base_pass(s, u, u == 0, False)
+
         def value_step(s):
             c, h = divmod(s, 2)
-            ve = bank(value_bank[s], "ve")
-            rhs, rhs_scale = xg_codes[c].bitcast(FP8X4), xg_scales[c]
-            for u in range(2):
-                t = 2 * h + u
-                nc.tensor.matmul_mx(
-                    out=by_slice(ve[:])[:, u, :],
-                    lhsT=wvd_codes[:, P * t : P * (t + 1)].bitcast(FP8X4),
-                    lhsT_scale=wvd_scales[:, P * t : P * (t + 1)],
-                    rhs=rhs,
-                    rhs_scale=rhs_scale,
-                    start=True,
-                    stop=False,
-                )
-                nc.tensor.matmul_mx(
-                    out=by_slice(ve[:])[:, u, :],
-                    lhsT=w4_words[:, 1, 2 * P * t : 2 * P * (t + 1)].bitcast(FP4X4),
-                    lhsT_scale=w4_scales[1][:, P * t : P * (t + 1)],
-                    rhs=rhs,
-                    rhs_scale=rhs_scale,
-                    start=False,
-                    stop=True,
-                )
+            if s in ve:
+                for u in range(2):
+                    change_pass(s, u, False, u == 1)
+            else:
+                ve[s] = bank(value_bank[s], "ve")
+                for u in range(2):
+                    change_pass(s, u, True, False)
+                    base_pass(s, u, False, True)
             result = y[c][:, 2 * h : 2 * h + 2, :]
-            nc.vector.tensor_tensor(result.rearrange("p u j -> p (u j)"), ve[:], gates[s], MULT)
+            nc.vector.tensor_tensor(result.rearrange("p u j -> p (u j)"), ve[s][:], gates[s], MULT)
             nc.sync.dma_start(out=out_rows[:, 2 * h : 2 * h + 2, c * CHUNK : (c + 1) * CHUNK], in_=result)
 
         def round_result(c, lo, hi, copy=nc.scalar.copy):
@@ -287,10 +299,13 @@ def tile_list_dl_sigP_kernel(
             key_product(s)
         xg_codes.append(keep.tile([P, CHUNK], U32, name="last_codes", tag="state2", align_bytes=64)[:])
         wvd_codes = keep.tile([P, N], U32, name="wvd_codes", tag="state3", align_bytes=64)
+        base_ahead(0)
+        base_ahead(1)
         quantize_picks(last)
         quantize_wvd()
         z[4] = keep.tile([P, BANK], F32, name="z4", tag="xg_bf0", align_bytes=64)[:]
-        gates[0] = keep.tile([P, BANK], F32, name="gate0", tag="state1", align_bytes=64)[:]
+        held = keep.tile([P, 3, BANK], F32, name="held", tag="state1", align_bytes=64)
+        gates[0], keys[4], keys[5] = held[:, 0, :], held[:, 1, :], held[:, 2, :]
         sigmoid(0)
         sigmoid(1)
         key_product_aside(4)
@@ -299,10 +314,11 @@ def tile_list_dl_sigP_kernel(
         key_product(6)
         for s in (3, 4, 6, 5):
             sigmoid(s)
-        first_bf = keep.tile([P, 2 * PACK * CHUNK], BF16, name="first_bf", tag="keys5", align_bytes=64)
+        value_step(0)
+        first_bf = keep.tile([P, 2 * PACK * CHUNK], BF16, name="first_bf", tag="state1", align_bytes=64)
         for c in range(2):
             y_bf[c] = first_bf[:, c * PACK * CHUNK : (c + 1) * PACK * CHUNK]
-        for s in range(5):
+        for s in range(1, 5):
             value_step(s)
             if s == 1:
                 round_result_aside(0, CHUNK)

@@ -102,7 +102,7 @@ def tile_list_dl_sigP_kernel(
         load_scales(1, wv4_scales)
         load_state(0)
         nc.sync.dma_start(out=wvd_raw[:], in_=wvd.rearrange("(p i) n -> p i n", i=PACK))
-        for s in (1, 2, 3, 4, 6, 5, 7):
+        for s in (1, 2, 3, 4, 5, 6, 7):
             load_state(s)
 
         warm = keep.tile([P, 1], F32, name="warm")
@@ -209,7 +209,7 @@ def tile_list_dl_sigP_kernel(
                 nc.vector.quantize_mx(out=wvd_codes[:, ns].bitcast(FP8X4), scales=wvd_scales[:, ns], in_=wvd_bf[h][:])
 
         y_scales = keep.tile([P, J], U8, name="y_scales", align_bytes=64)
-        y = [keep.tile([P, PACK, CHUNK], F32, name="y%d" % c) for c in range(chunks)]
+        y = [keep.tile([P, PACK, CHUNK], F32, name="y%d" % c)[:] for c in range(last)]
         y_bf = {c: keep.tile([P, PACK * CHUNK], BF16, name="y_bf%d" % c, align_bytes=64)[:] for c in range(2, chunks)}
         z = {s: keep.tile([P, BANK], F32, name="z%d" % s, align_bytes=64)[:] for s in range(steps) if s != 4}
         gates = {s: keep.tile([P, BANK], F32, name="gate%d" % s, align_bytes=64)[:] for s in range(1, steps - 1)}
@@ -297,13 +297,13 @@ def tile_list_dl_sigP_kernel(
 
         for s in range(4):
             key_product(s)
-        xg_codes.append(keep.tile([P, CHUNK], U32, name="last_codes", tag="state2", align_bytes=64)[:])
-        wvd_codes = keep.tile([P, N], U32, name="wvd_codes", tag="state3", align_bytes=64)
+        xg_codes.append(keep.tile([P, CHUNK], U32, name="last_codes", tag="state3", align_bytes=64)[:])
+        wvd_codes = keep.tile([P, N], U32, name="wvd_codes", tag="state2", align_bytes=64)
         base_ahead(0)
         base_ahead(1)
-        quantize_picks(last)
         quantize_wvd()
-        z[4] = keep.tile([P, BANK], F32, name="z4", tag="xg_bf0", align_bytes=64)[:]
+        quantize_picks(last)
+        z[4] = keep.tile([P, BANK], F32, name="z4", tag="xg_bf1", align_bytes=64)[:]
         held = keep.tile([P, 3, BANK], F32, name="held", tag="state1", align_bytes=64)
         gates[0], keys[4], keys[5] = held[:, 0, :], held[:, 1, :], held[:, 2, :]
         sigmoid(0)
@@ -311,9 +311,8 @@ def tile_list_dl_sigP_kernel(
         key_product_aside(4)
         sigmoid(2)
         key_product_aside(5)
-        key_product(6)
-        for s in (3, 4, 6, 5):
-            sigmoid(s)
+        sigmoid(3)
+        sigmoid(4)
         value_step(0)
         first_bf = keep.tile([P, 2 * PACK * CHUNK], BF16, name="first_bf", tag="state1", align_bytes=64)
         for c in range(2):
@@ -322,11 +321,17 @@ def tile_list_dl_sigP_kernel(
             value_step(s)
             if s == 1:
                 round_result_aside(0, CHUNK)
+            if s == 2:
+                key_product(6)
+                sigmoid(6)
+                sigmoid(5)
             if s == 3:
                 round_result_aside(1, ASIDE_Y)
                 round_result(1, ASIDE_Y, CHUNK)
         key_product(7)
-        gates[7] = keep.tile([P, BANK], F32, name="gate7", tag="z5", align_bytes=64)[:]
+        behind = keep.tile([P, PACK + 2, CHUNK], F32, name="behind", tag="z5", align_bytes=64)
+        y.append(behind[:, 0:PACK, :])
+        gates[7] = behind[:, PACK : PACK + 2, :].rearrange("p u j -> p (u j)")
         sigmoid(7)
         value_step(5)
         round_result(2, 0, CHUNK)

from contextlib import ExitStack

import concourse.mybir as mybir
from concourse.masks import make_identity

K, N, T, J = 512, 512, 2048, 1024
FLOPS = 3 * 2 * K * N * J

F32 = mybir.dt.float32
BF16 = mybir.dt.bfloat16
I32 = mybir.dt.int32
U32 = mybir.dt.uint32
U16 = mybir.dt.uint16
U8 = mybir.dt.uint8
FP8X4 = mybir.dt.float8_e4m3fn_x4
FP4X4 = mybir.dt.float4_e2m1fn_x4
MULT = mybir.AluOpType.mult
SIGMOID = mybir.ActivationFunctionType.Sigmoid

P = 128
PACK = 4
QUADRANTS = 4
LIST_ROWS = 16
BANK = 512
CHUNK = 256
HALF = CHUNK // 2
ASIDE_Y = 112
OWN_Y = 64
BLOCKS = J // P
REPEAT = 8


def weave(rows):
    return rows.rearrange("p t (pair e) -> p pair t e", e=2)


def woven(packed):
    return packed.rearrange("p (pair e t) -> p pair t e", e=2, t=PACK)


def tile_list_dl_sigP_kernel(
    tc, xT, wgt, wk_words, wk_scales, wv4_words, wv4_scales, wvd, st, offs, out_0, out_1, out_2
):
    nc = tc.nc
    chunks = J // CHUNK
    steps = 2 * chunks
    last = chunks - 1
    x_rows = xT.rearrange("(p i) token -> p i token", i=PACK)
    st_rows = st.rearrange("(p t) j -> p t j", t=PACK)
    out_rows = out_0.rearrange("(p t) j -> p t j", t=PACK)
    out_words = out_1[0].rearrange("p j i -> p (j i)").bitcast(I32)
    out_scales = out_2[0].bitcast(I32)

    with ExitStack() as ctx:
        keep = ctx.enter_context(tc.tile_pool(name="keep", bufs=1))
        ring = ctx.enter_context(tc.tile_pool(name="ring", bufs=chunks))
        psum = ctx.enter_context(tc.psum_pool(name="psum", bufs=1))

        def bank(number, name):
            return psum.tile([P, BANK], F32, name=name, tag="bank%d" % number)

        offsets = keep.tile([P, J // LIST_ROWS], U16, name="offsets")
        raw_words = keep.tile([P, 2, 2 * N], U8, name="raw_words")
        raw_scales = [keep.tile([P, N], U8, name="raw_scales%d" % w, align_bytes=64) for w in range(2)]
        planes = [keep.tile([P, T], F32, name="plane%d" % i) for i in range(PACK)]
        weight = [keep.tile([P, BANK], F32, name="weight%d" % h) for h in range(2)]
        weight_rows = keep.tile([P, P], F32, name="weight_rows")
        wvd_raw = keep.tile([P, PACK, N], F32, name="wvd_raw")
        identity = keep.tile([P, P], F32, name="identity")
        state = [keep.tile([P, BANK], F32, name="state%d" % s, align_bytes=64)[:] for s in range(steps)]

        for w in range(2):
            nc.gpsimd.memset(raw_scales[w][:].bitcast(I32), 0)
        make_identity(nc, identity[:])

        def load_scales(w, scales):
            for q in range(QUADRANTS):
                nc.sync.dma_start(
                    out=raw_scales[w][32 * q : 32 * q + 4, :].bitcast(I32),
                    in_=scales[0, 4 * q : 4 * q + 4, :].bitcast(I32),
                )

        def load_plane(i):
            nc.sync.dma_start(out=planes[i][:], in_=x_rows[:, i, :])

        def load_state(s):
            c, h = divmod(s, 2)
            nc.sync.dma_start(
                out=state[s].rearrange("p (t j) -> p t j", t=2),
                in_=st_rows[:, 2 * h : 2 * h + 2, c * CHUNK : (c + 1) * CHUNK],
            )

        nc.sync.dma_start(out=weight_rows[:], in_=wgt.rearrange("(a b) (r j) -> a b r j", b=REPEAT, j=P)[:, 0, :, :])
        load_plane(0)
        nc.sync.dma_start(offsets[:], offs)
        load_scales(0, wk_scales)
        load_plane(1)
        for w, words in enumerate((wk_words, wv4_words)):
            nc.sync.dma_start(out=raw_words[:, w, :].bitcast(I32), in_=words[0].bitcast(I32))
        for i in range(2, PACK):
            load_plane(i)
        load_scales(1, wv4_scales)
        load_state(0)
        nc.sync.dma_start(out=wvd_raw[:], in_=wvd.rearrange("(p i) n -> p i n", i=PACK))
        for s in (1, 2, 3, 4, 5, 6, 7):
            load_state(s)

        warm = keep.tile([P, 1], F32, name="warm")
        nc.vector.memset(warm[:], 0.0)
        warm_out = keep.tile([P, 1], F32, name="warm_out")
        nc.scalar.activation(out=warm_out[:], in_=warm[:], func=SIGMOID)

        turned = bank(4, "turned")
        nc.tensor.transpose(turned[:, 0:P], weight_rows[:], identity[:])
        by_block = turned[:, 0:P].rearrange("j (a r) -> j r a", r=BLOCKS)
        for c in range(chunks):
            spread = ring.tile([P, 2, P], F32, name="spread")
            nc.scalar.copy(
                out=spread[:].rearrange("j r (a x) -> j r a x", x=REPEAT),
                in_=by_block[:, 2 * c : 2 * c + 2, :].unsqueeze(3).to_broadcast([P, 2, P // REPEAT, REPEAT]),
            )
            turned_back = bank(c, "turned_back")
            for r in range(2):
                nc.tensor.transpose(turned_back[:, r * P : (r + 1) * P], spread[:, r, :], identity[:])
            nc.scalar.copy(out=weight[c // 2][:, c % 2 * CHUNK : (c % 2 + 1) * CHUNK], in_=turned_back[:, 0:CHUNK])

        w4_words = keep.tile([P, 2, 2 * N], U8, name="w4_words", align_bytes=64)
        w4_scales = {0: keep.tile([P, N], U8, name="w4_scales0", align_bytes=64)}

        def deal_words():
            nc.scalar.copy(
                out=w4_words[:].bitcast(U16).rearrange("p w (t m) -> p w t m", t=PACK),
                in_=raw_words[:].bitcast(U16).rearrange("p w (m t) -> p w t m", t=PACK),
            )

        def deal_scales(w, copy):
            copy(
                out=w4_scales[w][:].rearrange("p (t m) -> p t m", t=PACK),
                in_=raw_scales[w][:].rearrange("p (m t) -> p t m", t=PACK),
            )

        early = keep.tile([P, 2, J], F32, name="early")
        shared = keep.tile([P, 3, CHUNK], F32, name="shared")
        pairs = {c: keep.tile([P, 2, CHUNK], F32, name="pair%d" % c)[:] for c in (0, 2)}
        pairs[1] = shared[:, 0:2, :]
        pairs[last] = shared[:, 0:3:2, :]

        def gather(out, i, j0, j1):
            nc.vector.tensor_tensor(
                out,
                planes[i][:].indirect(offsets[:, j0 // LIST_ROWS : j1 // LIST_ROWS]),
                weight[j0 // BANK][:, j0 % BANK : j0 % BANK + j1 - j0],
                MULT,
            )

        def gather_late(i, c):
            gather(pairs[c][:, i - 2, :], i, c * CHUNK, (c + 1) * CHUNK)

        xg_codes = [keep.tile([P, CHUNK], U32, name="xg_codes%d" % c, align_bytes=64)[:] for c in range(last)]
        xg_scales = [keep.tile([P, CHUNK], U8, name="xg_scales%d" % c, align_bytes=64)[:] for c in range(chunks)]
        xg_bf = [keep.tile([P, PACK * CHUNK], BF16, name="xg_bf%d" % c, align_bytes=64) for c in range(chunks)]

        def round_picks(c, i, pair):
            nc.scalar.copy(out=woven(xg_bf[c][:])[:, :, i : i + 2, :], in_=weave(pair))

        def round_picks_aside(c, i, pair):
            nc.gpsimd.tensor_copy(
                out=xg_bf[c][:].rearrange("p (j t) -> p j t", t=PACK)[:, :, i : i + 2],
                in_=pair.rearrange("p t j -> p j t"),
            )

        def quantize_picks(c):
            nc.vector.quantize_mx(out=xg_codes[c].bitcast(FP8X4), scales=xg_scales[c], in_=xg_bf[c][:])

        deal_words()
        for i in range(2):
            for j0 in range(0, J, BANK):
                gather(early[:, i, j0 : j0 + BANK], i, j0, j0 + BANK)
        for c in range(chunks):
            round_picks(c, 0, early[:, :, c * CHUNK : (c + 1) * CHUNK])
        for c in range(last):
            gather_late(2, c)
        for c in range(chunks):
            gather_late(3, c)
        for c in range(last):
            round_picks(c, 2, pairs[c])
        deal_scales(0, nc.vector.tensor_copy)
        quantize_picks(0)
        quantize_picks(1)
        gather_late(2, last)
        quantize_picks(2)
        round_picks_aside(last, 2, pairs[last])
        w4_scales[1] = keep.tile([P, N], U8, name="w4_scales1", tag="xg_bf2", align_bytes=64)
        deal_scales(1, nc.gpsimd.tensor_copy)

        wvd_bf = [
            keep.tile([P, 2 * N], BF16, name="wvd_bf%d" % h, tag="xg_bf%d" % h, align_bytes=64) for h in range(2)
        ]
        wvd_scales = keep.tile([P, N], U8, name="wvd_scales", align_bytes=64)
        for h in range(2):
            nc.scalar.copy(
                out=wvd_bf[h][:].rearrange("p (u m i) -> p m i u", u=2, i=PACK),
                in_=wvd_raw[:].rearrange("p i (m h u) -> p h m i u", h=2, u=2)[:, h],
            )

        def quantize_wvd():
            for h in range(2):
                ns = slice(h * N // 2, (h + 1) * N // 2)
                nc.vector.quantize_mx(out=wvd_codes[:, ns].bitcast(FP8X4), scales=wvd_scales[:, ns], in_=wvd_bf[h][:])

        y_scales = keep.tile([P, J], U8, name="y_scales", align_bytes=64)
        y = [keep.tile([P, PACK, CHUNK], F32, name="y%d" % c)[:] for c in range(last)]
        y_bf = {c: keep.tile([P, PACK * CHUNK], BF16, name="y_bf%d" % c, align_bytes=64)[:] for c in range(2, chunks)}
        z = {s: keep.tile([P, BANK], F32, name="z%d" % s, align_bytes=64)[:] for s in range(steps) if s != 4}
        gates = {s: keep.tile([P, BANK], F32, name="gate%d" % s, align_bytes=64)[:] for s in range(1, steps - 1)}
        keys = {}
        key_bank = (0, 1, 2, 3, 4, 5, 0, 1)
        value_bank = (1, 2, 3, 6, 7, 4, 5, 0)
        ve = {}

        def by_slice(flat):
            return flat.rearrange("p (u j) -> p u j", u=2)

        def key_matmuls(s):
            c, h = divmod(s, 2)
            ke = bank(key_bank[s], "ke")
            for u in range(2):
                t = 2 * h + u
                nc.tensor.matmul_mx(
                    out=by_slice(ke[:])[:, u, :],
                    lhsT=w4_words[:, 0, 2 * P * t : 2 * P * (t + 1)].bitcast(FP4X4),
                    lhsT_scale=w4_scales[0][:, P * t : P * (t + 1)],
                    rhs=xg_codes[c].bitcast(FP8X4),
                    rhs_scale=xg_scales[c],
                    start=True,
                    stop=True,
                )
            return ke[:]

        def key_product(s):
            nc.vector.tensor_tensor(z[s], key_matmuls(s), state[s], MULT)

        def key_product_aside(s):
            nc.scalar.copy(out=keys[s], in_=key_matmuls(s))
            nc.gpsimd.tensor_tensor(z[s], keys[s], state[s], MULT)

        def sigmoid(s):
            nc.scalar.activation(out=gates[s], in_=z[s], func=SIGMOID)

        def value_pass(s, u, words, scales, start, stop):
            c, h = divmod(s, 2)
            nc.tensor.matmul_mx(
                out=by_slice(ve[s][:])[:, u, :],
                lhsT=words,
                lhsT_scale=scales[:, P * (2 * h + u) : P * (2 * h + u + 1)],
                rhs=xg_codes[c].bitcast(FP8X4),
                rhs_scale=xg_scales[c],
                start=start,
                stop=stop,
            )

        def base_pass(s, u, start, stop):
            t = 2 * (s % 2) + u
            value_pass(s, u, w4_words[:, 1, 2 * P * t : 2 * P * (t + 1)].bitcast(FP4X4), w4_scales[1], start, stop)

        def change_pass(s, u, start, stop):
            t = 2 * (s % 2) + u
            value_pass(s, u, wvd_codes[:, P * t : P * (t + 1)].bitcast(FP8X4), wvd_scales, start, stop)

        def base_ahead(s):
            ve[s] = bank(value_bank[s], "ve")
            for u in range(2):
                base_pass(s, u, u == 0, False)

        def value_step(s):
            c, h = divmod(s, 2)
            if s in ve:
                for u in range(2):
                    change_pass(s, u, False, u == 1)
            else:
                ve[s] = bank(value_bank[s], "ve")
                for u in range(2):
                    change_pass(s, u, True, False)
                    base_pass(s, u, False, True)
            result = y[c][:, 2 * h : 2 * h + 2, :]
            nc.vector.tensor_tensor(result.rearrange("p u j -> p (u j)"), ve[s][:], gates[s], MULT)
            nc.sync.dma_start(out=out_rows[:, 2 * h : 2 * h + 2, c * CHUNK : (c + 1) * CHUNK], in_=result)

        def round_result(c, lo, hi, copy=nc.scalar.copy):
            copy(out=woven(y_bf[c][:, PACK * lo : PACK * hi]), in_=weave(y[c][:, :, lo:hi]))

        def round_result_aside(c, hi):
            nc.gpsimd.tensor_copy(
                out=y_bf[c][:, 0 : PACK * hi].rearrange("p (j t) -> p j t", t=PACK),
                in_=y[c][:, :, 0:hi].rearrange("p t j -> p j t"),
            )

        for s in range(4):
            key_product(s)
        xg_codes.append(keep.tile([P, CHUNK], U32, name="last_codes", tag="state3", align_bytes=64)[:])
        wvd_codes = keep.tile([P, N], U32, name="wvd_codes", tag="state2", align_bytes=64)
        base_ahead(0)
        base_ahead(1)
        quantize_wvd()
        quantize_picks(last)
        z[4] = keep.tile([P, BANK], F32, name="z4", tag="xg_bf1", align_bytes=64)[:]
        held = keep.tile([P, 3, BANK], F32, name="held", tag="state1", align_bytes=64)
        gates[0], keys[4], keys[5] = held[:, 0, :], held[:, 1, :], held[:, 2, :]
        sigmoid(0)
        sigmoid(1)
        key_product_aside(4)
        sigmoid(2)
        key_product_aside(5)
        sigmoid(3)
        sigmoid(4)
        value_step(0)
        first_bf = keep.tile([P, 2 * PACK * CHUNK], BF16, name="first_bf", tag="state1", align_bytes=64)
        for c in range(2):
            y_bf[c] = first_bf[:, c * PACK * CHUNK : (c + 1) * PACK * CHUNK]
        for s in range(1, 5):
            value_step(s)
            if s == 1:
                round_result_aside(0, CHUNK)
            if s == 2:
                key_product(6)
                sigmoid(6)
                sigmoid(5)
            if s == 3:
                round_result_aside(1, ASIDE_Y)
                round_result(1, ASIDE_Y, CHUNK)
        key_product(7)
        behind = keep.tile([P, PACK + 2, CHUNK], F32, name="behind", tag="z5", align_bytes=64)
        y.append(behind[:, 0:PACK, :])
        gates[7] = behind[:, PACK : PACK + 2, :].rearrange("p u j -> p (u j)")
        sigmoid(7)
        value_step(5)
        round_result(2, 0, CHUNK)
        value_step(6)
        value_step(7)
        round_result(last, 0, HALF)
        round_result(last, HALF, CHUNK - OWN_Y)

        y_codes = keep.tile([P, J], U32, name="y_codes", tag="z7", align_bytes=64)

        def quantize_result(c, lo, hi):
            js = slice(c * CHUNK + lo, c * CHUNK + hi)
            nc.vector.quantize_mx(
                out=y_codes[:, js].bitcast(FP8X4), scales=y_scales[:, js], in_=y_bf[c][:, PACK * lo : PACK * hi]
            )

        for c in range(last):
            quantize_result(c, 0, CHUNK)
        nc.sync.dma_start(out=out_words[:, 0 : last * CHUNK], in_=y_codes[:, 0 : last * CHUNK].bitcast(I32))
        round_result(last, CHUNK - OWN_Y, CHUNK, nc.vector.tensor_copy)
        quantize_result(last, 0, HALF)
        quantize_result(last, HALF, CHUNK)

        nc.scalar.dma_start(out=out_words[:, last * CHUNK : J], in_=y_codes[:, last * CHUNK : J].bitcast(I32))
        for q in range(QUADRANTS):
            queue = nc.sync if q % 2 == 0 else nc.scalar
            queue.dma_start(out=out_scales[4 * q : 4 * q + 4, :], in_=y_scales[32 * q : 32 * q + 4, :].bitcast(I32))
